import numpy as np
import ml_dtypes


def mxq(x, axis, fmt="e4m3"):
    dtype, down = {"e4m3": (ml_dtypes.float8_e4m3fn, 7), "e5m2": (ml_dtypes.float8_e5m2, 14)}[fmt]
    v = np.moveaxis(np.asarray(x, np.float32).astype(ml_dtypes.bfloat16).astype(np.float64), axis, -1)
    blocks = v.reshape(v.shape[:-1] + (-1, 32))
    amax = np.abs(blocks).max(-1, keepdims=True)
    byte = np.maximum(np.where(amax > 0, np.frexp(amax)[1] - 1 + 127, 0) - down, 1)
    scale = np.exp2(byte - 127.0)
    codes = (blocks / scale).astype(np.float32).astype(dtype).astype(np.float64)
    return np.moveaxis((codes * scale).reshape(v.shape), -1, axis)


WIDE = False


def mx_kscale(k):
    if not WIDE:
        return np.ones(k)
    levels = np.array([10, -10, 5, -5, 0])
    if k % 512:
        return np.exp2(np.random.permutation(np.resize(levels, k // 32))).repeat(32)
    a = np.empty((k // 512, 16))
    for p in range(k // 512):
        a[p, :8] = np.random.permutation(np.resize(levels, 8))
        for g in range(8):
            far = levels[np.abs(levels - a[p, g]) >= 10]
            a[p, g + 8] = far[np.random.randint(len(far))]
    return np.exp2(a.ravel()).repeat(32)


def f64(x):
    return np.asarray(x).astype(np.float64)


def striped(idx):
    return np.tile(idx.reshape(-1, 16).T, (8, 1)).astype(np.uint16)


def unstriped(offs):
    return offs[:16].T.reshape(-1).astype(np.int64)


K, T, D, S, V, N = 1024, 1024, 8, 4096, 512, 128


def setup_inputs():
    n = np.random.standard_normal
    s = mx_kscale(K)[:, None]
    return {
        "xT": (n((K, T)) * s).astype(np.float32),
        "w": (n((K, N)) / np.sqrt(K) / s).astype(np.float32),
        "b": (0.3 * n((N, 1))).astype(np.float32),
        "gate": np.tile(np.random.uniform(0.2, 1.0, (D, 1, V)) / np.sqrt(D), (1, N, 1)).astype(np.float32),
        "pos1": striped(np.random.permutation(T)[:V]),
        "pos2": striped(np.random.permutation(T)[:V]),
        "pos3": striped(np.random.permutation(T)[:V]),
        "pos4": striped(np.random.permutation(T)[:V]),
        "pos5": striped(np.random.permutation(T)[:V]),
        "pos6": striped(np.random.permutation(T)[:V]),
        "pos7": striped(np.random.permutation(T)[:V]),
        "pos8": striped(np.random.permutation(T)[:V]),
    }


def reference(xT, w, b, gate, pos1, pos2, pos3, pos4, pos5, pos6, pos7, pos8):
    y = mxq(f64(w), 0, "e4m3").T @ mxq(f64(xT), 0, "e4m3")
    y = y + f64(b)
    return sum(f64(gate[d]) * y[:, unstriped(p)] for d, p in enumerate((pos1, pos2, pos3, pos4, pos5, pos6, pos7, pos8)))

@@ -1,0 +1,169 @@
+from contextlib import ExitStack
+
+import concourse.mybir as mybir
+from concourse.masks import make_identity
+
+K, T, D, V, M = 1024, 1024, 8, 512, 128
+P = 128
+PACK = 4
+K_PASS = P * PACK
+PASSES = K // K_PASS
+
+FLOPS = 2 * K * T * M + 2 * D * V * M
+
+F32 = mybir.dt.float32
+BF16 = mybir.dt.bfloat16
+U32 = mybir.dt.uint32
+U16 = mybir.dt.uint16
+U8 = mybir.dt.uint8
+FP8X4 = mybir.dt.float8_e4m3fn_x4
+MULT = mybir.AluOpType.mult
+ADD = mybir.AluOpType.add
+IDENTITY = mybir.ActivationFunctionType.Identity
+
+
+LOADS = ((0, 0, 1024), (1, 0, 512), (1, 512, 256), (1, 768, 256))
+RANGES = ((0, 512), (512, 256), (768, 128), (896, 128))
+UNITS = ((0, 0, 512, 8), (0, 512, 512, 8), (1, 0, 512, 9), (1, 512, 256, 11))
+LAST = ((1, 768, 128, 16), (1, 896, 128, 16))
+
+
+def tile_picked_agg_lin_bias_sub_l_kernel(
+    tc, xT, w, b, gate, pos1, pos2, pos3, pos4, pos5, pos6, pos7, pos8, out
+):
+    nc = tc.nc
+    lists = (pos1, pos2, pos3, pos4, pos5, pos6, pos7, pos8)
+    with ExitStack() as ctx:
+        keep = ctx.enter_context(tc.tile_pool(name="keep", bufs=1))
+        psum = ctx.enter_context(tc.psum_pool(name="psum", bufs=1))
+
+        bias = keep.tile([P, 1], F32, name="bias")
+        nc.scalar.dma_start(out=bias[:], in_=b)
+        ident = keep.tile([P, P], F32, name="ident")
+        make_identity(nc, ident[:])
+
+        w_raw = keep.tile([P, PASSES, PACK, M], F32, name="w_raw")
+        nc.sync.dma_start(out=w_raw[:], in_=w.rearrange("(c p j) m -> p c j m", c=PASSES, j=PACK))
+        raws = []
+        for c, t0, n in LOADS:
+            raw = keep.tile([P, PACK, n], F32, name=f"raw{c}_{t0}")
+            nc.sync.dma_start(
+                out=raw[:],
+                in_=xT[c * K_PASS : (c + 1) * K_PASS, t0 : t0 + n].rearrange("(p j) w -> p j w", j=PACK),
+            )
+            raws.append((c, t0, n, raw))
+        offs = []
+        gates = []
+        for d in range(D):
+            off = keep.tile([P, V // 16], U16, name=f"off{d}")
+            nc.sync.dma_start(off[:], lists[d])
+            offs.append(off)
+            g = keep.tile([P, V], F32, name=f"gate{d}")
+            nc.sync.dma_start(out=g[:], in_=gate[d])
+            gates.append(g)
+
+        def interleave(copy, grouped, raw):
+            copy(
+                out=grouped.rearrange("p (g i) j -> p g j i", i=4),
+                in_=raw.rearrange("p j (g i) -> p g j i", i=4),
+            )
+
+        w_grp = keep.tile([P, PASSES, M, PACK], BF16, name="w_grp", align_bytes=64)
+        w_codes = keep.tile([P, PASSES * M], U32, name="w_codes", align_bytes=64)
+        w_scales = keep.tile([P, PASSES * M], U8, name="w_scales", align_bytes=64)
+        interleave(nc.vector.tensor_copy, w_grp[:, 0], w_raw[:, 0])
+        interleave(nc.scalar.copy, w_grp[:, 1], w_raw[:, 1])
+        nc.vector.quantize_mx(
+            out=w_codes[:].bitcast(FP8X4), scales=w_scales[:], in_=w_grp[:].rearrange("p c m j -> p (c m j)")
+        )
+
+        y = keep.tile([P, T], F32, name="y")
+        x_codes = keep.tile([P, PASSES, T], U32, name="x_codes", align_bytes=64)
+        x_scales = keep.tile([P, PASSES, T], U8, name="x_scales", align_bytes=64)
+        banks = {}
+        for t0, n in RANGES:
+            bank = psum.tile([P, n], F32, name=f"y{t0}")
+            banks[t0] = bank
+
+        def copies(c, t0, n, share):
+            raw = [r[:, :, t0 - s : t0 - s + n] for (q, s, m, r) in raws if q == c and s <= t0 < s + m][0]
+            grp = keep.tile([P, n, PACK], BF16, name=f"grp{c}_{t0}", align_bytes=64)
+            cut = n * share // 16
+            if cut < n:
+                interleave(nc.scalar.copy, grp[:, cut:], raw[:, :, cut:])
+            interleave(nc.vector.tensor_copy, grp[:, :cut], raw[:, :, :cut])
+            return grp
+
+        def product(c, t0, n, grp):
+            nc.vector.quantize_mx(
+                out=x_codes[:, c, t0 : t0 + n].bitcast(FP8X4),
+                scales=x_scales[:, c, t0 : t0 + n],
+                in_=grp[:].rearrange("p w j -> p (w j)"),
+            )
+            for r0, rn in RANGES:
+                if t0 <= r0 < t0 + n:
+                    nc.tensor.matmul_mx(
+                        out=banks[r0][:],
+                        lhsT=w_codes[:, c * M : (c + 1) * M].bitcast(FP8X4),
+                        lhsT_scale=w_scales[:, c * M : (c + 1) * M],
+                        rhs=x_codes[:, c, r0 : r0 + rn].bitcast(FP8X4),
+                        rhs_scale=x_scales[:, c, r0 : r0 + rn],
+                        start=(c == 0),
+                        stop=(c == PASSES - 1),
+                    )
+
+        def bring(t0, n):
+            nc.scalar.activation(out=y[:, t0 : t0 + n], in_=banks[t0][:], func=IDENTITY, bias=bias[:])
+
+        for c, t0, n, share in UNITS:
+            grp = copies(c, t0, n, share)
+            product(c, t0, n, grp)
+        grps = [copies(*unit) for unit in LAST]
+        for t0, n in RANGES[:2]:
+            bring(t0, n)
+        for (c, t0, n, share), grp in zip(LAST, grps):
+            product(c, t0, n, grp)
+        bring(*RANGES[2])
+        t0, n = RANGES[3]
+        nc.vector.tensor_scalar(out=y[:, t0 : t0 + n], in0=banks[t0][:], scalar1=bias[:], scalar2=None, op0=ADD)
+
+        prods = []
+        accs = []
+        for d in range(D):
+            prod = keep.tile([P, V], F32, name=f"prod{d}")
+            prods.append(prod)
+        for i in range(V // P):
+            acc = psum.tile([P, P], F32, name=f"acc{i}")
+            accs.append(acc)
+        backs = [psum.tile([P, 2 * P], F32, name=f"back{h}", tag=("y0", "y512")[h]) for h in range(2)]
+        turned = keep.tile([P, V], F32, name="turned")
+        res = keep.tile([P, V], F32, name="res")
+
+        def gather(d, lo, hi):
+            nc.vector.tensor_tensor(
+                prods[d][:, lo:hi], y[:].indirect(offs[d][:, lo // 16 : hi // 16]), gates[d][:, lo:hi], MULT
+            )
+
+        def add_up(d, i, last):
+            nc.tensor.matmul(
+                accs[i][:], prods[d][:, i * P : (i + 1) * P], ident[:], start=(d == 0), stop=(d == last), is_transpose=True
+            )
+
+        for d in range(D - 2):
+            gather(d, 0, V)
+            for i in range(4):
+                add_up(d, i, D - 2)
+        for h in range(2):
+            gather(D - 2, 2 * h * P, 2 * (h + 1) * P)
+            for i in (2 * h, 2 * h + 1):
+                add_up(D - 2, i, D - 2)
+        for i in range(4):
+            nc.scalar.copy(out=turned[:, i * P : (i + 1) * P], in_=accs[i][:])
+        for i in range(4):
+            nc.tensor.transpose(backs[i // 2][:, i % 2 * P : (i % 2 + 1) * P], turned[:, i * P : (i + 1) * P], ident[:])
+        for h in range(2):
+            gather(D - 1, 2 * h * P, 2 * (h + 1) * P)
+        for h in range(2):
+            lo, hi = 2 * h * P, 2 * (h + 1) * P
+            nc.vector.tensor_tensor(res[:, lo:hi], prods[7][:, lo:hi], backs[h][:], ADD)
+            nc.sync.dma_start(out=out[:, lo:hi], in_=res[:, lo:hi])

@@ -22,10 +22,9 @@ ADD = mybir.AluOpType.add
 IDENTITY = mybir.ActivationFunctionType.Identity
 
 
-LOADS = ((0, 0, 1024), (1, 0, 512), (1, 512, 256), (1, 768, 256))
 RANGES = ((0, 512), (512, 256), (768, 128), (896, 128))
-UNITS = ((0, 0, 512, 8), (0, 512, 512, 8), (1, 0, 512, 9), (1, 512, 256, 11))
-LAST = ((1, 768, 128, 16), (1, 896, 128, 16))
+UNITS = ((0, 0, 512), (0, 512, 512), (1, 0, 512), (1, 512, 256), (1, 768, 256))
+LATE = ((0, 512), (512, 256), (768, 256))
 
 
 def tile_picked_agg_lin_bias_sub_l_kernel(
@@ -42,16 +41,16 @@ def tile_picked_agg_lin_bias_sub_l_kernel(
         ident = keep.tile([P, P], F32, name="ident")
         make_identity(nc, ident[:])
 
+        x_rows = xT.rearrange("(c p j) t -> c p j t", c=PASSES, j=PACK)
+        raw0 = keep.tile([P, PACK, T], F32, name="raw0")
+        nc.sync.dma_start(out=raw0[:], in_=x_rows[0])
         w_raw = keep.tile([P, PASSES, PACK, M], F32, name="w_raw")
         nc.sync.dma_start(out=w_raw[:], in_=w.rearrange("(c p j) m -> p c j m", c=PASSES, j=PACK))
-        raws = []
-        for c, t0, n in LOADS:
-            raw = keep.tile([P, PACK, n], F32, name=f"raw{c}_{t0}")
-            nc.sync.dma_start(
-                out=raw[:],
-                in_=xT[c * K_PASS : (c + 1) * K_PASS, t0 : t0 + n].rearrange("(p j) w -> p j w", j=PACK),
-            )
-            raws.append((c, t0, n, raw))
+        late = {}
+        for t0, n in LATE:
+            raw = keep.tile([P, PACK, n], F32, name=f"late{t0}")
+            nc.sync.dma_start(out=raw[:], in_=x_rows[1][:, :, t0 : t0 + n])
+            late[t0] = raw
         offs = []
         gates = []
         for d in range(D):
@@ -68,62 +67,80 @@ def tile_picked_agg_lin_bias_sub_l_kernel(
                 in_=raw.rearrange("p j (g i) -> p g j i", i=4),
             )
 
+        y = keep.tile([P, T], F32, name="y")
         w_grp = keep.tile([P, PASSES, M, PACK], BF16, name="w_grp", align_bytes=64)
         w_codes = keep.tile([P, PASSES * M], U32, name="w_codes", align_bytes=64)
         w_scales = keep.tile([P, PASSES * M], U8, name="w_scales", align_bytes=64)
-        interleave(nc.vector.tensor_copy, w_grp[:, 0], w_raw[:, 0])
-        interleave(nc.scalar.copy, w_grp[:, 1], w_raw[:, 1])
-        nc.vector.quantize_mx(
-            out=w_codes[:].bitcast(FP8X4), scales=w_scales[:], in_=w_grp[:].rearrange("p c m j -> p (c m j)")
-        )
+        grp, x_codes, x_scales = {}, {}, {}
+        for c, t0, n in UNITS:
+            grp[c, t0] = keep.tile([P, n, PACK], BF16, name=f"grp{c}_{t0}", align_bytes=64)
+            x_codes[c, t0] = keep.tile([P, n], U32, name=f"x_codes{c}_{t0}", align_bytes=64)
+            x_scales[c, t0] = keep.tile([P, n], U8, name=f"x_scales{c}_{t0}", align_bytes=64)
 
-        y = keep.tile([P, T], F32, name="y")
-        x_codes = keep.tile([P, PASSES, T], U32, name="x_codes", align_bytes=64)
-        x_scales = keep.tile([P, PASSES, T], U8, name="x_scales", align_bytes=64)
+        def part(tiles, c, lo, hi):
+            t0 = max(s for q, s, n in UNITS if q == c and s <= lo)
+            return tiles[c, t0][:, lo - t0 : hi - t0]
+
         banks = {}
         for t0, n in RANGES:
             bank = psum.tile([P, n], F32, name=f"y{t0}")
             banks[t0] = bank
 
-        def copies(c, t0, n, share):
-            raw = [r[:, :, t0 - s : t0 - s + n] for (q, s, m, r) in raws if q == c and s <= t0 < s + m][0]
-            grp = keep.tile([P, n, PACK], BF16, name=f"grp{c}_{t0}", align_bytes=64)
-            cut = n * share // 16
-            if cut < n:
-                interleave(nc.scalar.copy, grp[:, cut:], raw[:, :, cut:])
-            interleave(nc.vector.tensor_copy, grp[:, :cut], raw[:, :, :cut])
-            return grp
-
-        def product(c, t0, n, grp):
+        def quantize(c, t0, n):
             nc.vector.quantize_mx(
-                out=x_codes[:, c, t0 : t0 + n].bitcast(FP8X4),
-                scales=x_scales[:, c, t0 : t0 + n],
-                in_=grp[:].rearrange("p w j -> p (w j)"),
+                out=part(x_codes, c, t0, t0 + n).bitcast(FP8X4),
+                scales=part(x_scales, c, t0, t0 + n),
+                in_=part(grp, c, t0, t0 + n).rearrange("p w j -> p (w j)"),
             )
-            for r0, rn in RANGES:
-                if t0 <= r0 < t0 + n:
-                    nc.tensor.matmul_mx(
-                        out=banks[r0][:],
-                        lhsT=w_codes[:, c * M : (c + 1) * M].bitcast(FP8X4),
-                        lhsT_scale=w_scales[:, c * M : (c + 1) * M],
-                        rhs=x_codes[:, c, r0 : r0 + rn].bitcast(FP8X4),
-                        rhs_scale=x_scales[:, c, r0 : r0 + rn],
-                        start=(c == 0),
-                        stop=(c == PASSES - 1),
-                    )
+
+        def multiply(c, r0, lo, hi):
+            nc.tensor.matmul_mx(
+                out=banks[r0][:],
+                lhsT=w_codes[:, c * M : (c + 1) * M].bitcast(FP8X4),
+                lhsT_scale=w_scales[:, c * M : (c + 1) * M],
+                rhs=part(x_codes, c, lo, hi).bitcast(FP8X4),
+                rhs_scale=part(x_scales, c, lo, hi),
+                start=(c == 0),
+                stop=(c == PASSES - 1),
+            )
 
         def bring(t0, n):
             nc.scalar.activation(out=y[:, t0 : t0 + n], in_=banks[t0][:], func=IDENTITY, bias=bias[:])
 
-        for c, t0, n, share in UNITS:
-            grp = copies(c, t0, n, share)
-            product(c, t0, n, grp)
-        grps = [copies(*unit) for unit in LAST]
-        for t0, n in RANGES[:2]:
+        def late_nodes(copy, t0, lo, hi):
+            interleave(copy, part(grp, 1, lo, hi), late[t0][:, :, lo - t0 : hi - t0])
+
+        vec, sca = nc.vector.tensor_copy, nc.scalar.copy
+        interleave(vec, part(grp, 0, 0, 368), raw0[:, :, 0:368])
+        interleave(sca, part(grp, 0, 368, 512), raw0[:, :, 368:512])
+        interleave(sca, part(grp, 0, 512, 768), raw0[:, :, 512:768])
+        interleave(sca, part(grp, 0, 768, T), raw0[:, :, 768:T])
+        interleave(vec, w_grp[:, 0], w_raw[:, 0])
+        interleave(vec, w_grp[:, 1], w_raw[:, 1])
+        quantize(0, 0, 512)
+        nc.vector.quantize_mx(
+            out=w_codes[:].bitcast(FP8X4), scales=w_scales[:], in_=w_grp[:].rearrange("p c m j -> p (c m j)")
+        )
+        quantize(0, 512, 256)
+        quantize(0, 768, 256)
+        for r0, rn in RANGES:
+            multiply(0, r0, r0, r0 + rn)
+        late_nodes(vec, 0, 0, 256)
+        late_nodes(sca, 0, 256, 512)
+        quantize(1, 0, 256)
+        quantize(1, 256, 256)
+        multiply(1, 0, 0, 512)
+        late_nodes(vec, 512, 512, 640)
+        late_nodes(sca, 512, 640, 768)
+        quantize(1, 512, 256)
+        multiply(1, 512, 512, 768)
+        late_nodes(vec, 768, 768, 944)
+        late_nodes(sca, 768, 944, T)
+        quantize(1, 768, 256)
+        multiply(1, 768, 768, 896)
+        multiply(1, 896, 896, T)
+        for t0, n in RANGES[:3]:
             bring(t0, n)
-        for (c, t0, n, share), grp in zip(LAST, grps):
-            product(c, t0, n, grp)
-        bring(*RANGES[2])
         t0, n = RANGES[3]
         nc.vector.tensor_scalar(out=y[:, t0 : t0 + n], in0=banks[t0][:], scalar1=bias[:], scalar2=None, op0=ADD)
 

@@ -63,8 +63,8 @@ def tile_picked_agg_lin_bias_sub_l_kernel(
 
         def interleave(copy, grouped, raw):
             copy(
-                out=grouped.rearrange("p (g i) j -> p g j i", i=4),
-                in_=raw.rearrange("p j (g i) -> p g j i", i=4),
+                out=grouped.rearrange("p (g i) j -> p g j i", i=2),
+                in_=raw.rearrange("p j (g i) -> p g j i", i=2),
             )
 
         y = keep.tile([P, T], F32, name="y")

@@ -24,7 +24,6 @@ IDENTITY = mybir.ActivationFunctionType.Identity
 
 RANGES = ((0, 512), (512, 256), (768, 128), (896, 128))
 UNITS = ((0, 0, 512), (0, 512, 512), (1, 0, 512), (1, 512, 256), (1, 768, 256))
-LATE = ((0, 512), (512, 256), (768, 256))
 
 
 def tile_picked_agg_lin_bias_sub_l_kernel(
@@ -36,21 +35,32 @@ def tile_picked_agg_lin_bias_sub_l_kernel(
         keep = ctx.enter_context(tc.tile_pool(name="keep", bufs=1))
         psum = ctx.enter_context(tc.psum_pool(name="psum", bufs=1))
 
-        bias = keep.tile([P, 1], F32, name="bias")
-        nc.scalar.dma_start(out=bias[:], in_=b)
         ident = keep.tile([P, P], F32, name="ident")
         make_identity(nc, ident[:])
 
         x_rows = xT.rearrange("(c p j) t -> c p j t", c=PASSES, j=PACK)
-        raw0 = keep.tile([P, PACK, T], F32, name="raw0")
-        nc.sync.dma_start(out=raw0[:], in_=x_rows[0])
-        w_raw = keep.tile([P, PASSES, PACK, M], F32, name="w_raw")
-        nc.sync.dma_start(out=w_raw[:], in_=w.rearrange("(c p j) m -> p c j m", c=PASSES, j=PACK))
-        late = {}
-        for t0, n in LATE:
-            raw = keep.tile([P, PACK, n], F32, name=f"late{t0}")
-            nc.sync.dma_start(out=raw[:], in_=x_rows[1][:, :, t0 : t0 + n])
-            late[t0] = raw
+        w_rows = w.rearrange("(c p j) m -> p c j m", c=PASSES, j=PACK)
+        raws = []
+        w_raws = {}
+
+        def load_x(c, j0, j1, t0, t1, tag=None):
+            raw = keep.tile([P, j1 - j0, t1 - t0], F32, name=f"raw{c}_{j0}_{t0}", tag=tag or f"raw{c}_{j0}_{t0}")
+            nc.sync.dma_start(out=raw[:], in_=x_rows[c][:, j0:j1, t0:t1])
+            raws.append((c, j0, j1, t0, t1, raw))
+
+        def load_w(c0, c1):
+            raw = keep.tile([P, c1 - c0, PACK, M], F32, name=f"w_raw{c0}")
+            nc.sync.dma_start(out=raw[:], in_=w_rows[:, c0:c1])
+            for c in range(c0, c1):
+                w_raws[c] = raw[:, c - c0]
+
+        bias = keep.tile([P, 1], F32, name="bias")
+        load_x(0, 0, 4, 0, T)
+        load_w(0, 2)
+        load_x(1, 0, 4, 0, 512)
+        load_x(1, 0, 4, 512, 768)
+        load_x(1, 0, 4, 768, T)
+        nc.sync.dma_start(out=bias[:], in_=b)
         offs = []
         gates = []
         for d in range(D):
@@ -93,56 +103,71 @@ def tile_picked_agg_lin_bias_sub_l_kernel(
                 in_=part(grp, c, t0, t0 + n).rearrange("p w j -> p (w j)"),
             )
 
-        def multiply(c, r0, lo, hi):
+        def quantize_w(c0, c1):
+            nc.vector.quantize_mx(
+                out=w_codes[:, c0 * M : c1 * M].bitcast(FP8X4),
+                scales=w_scales[:, c0 * M : c1 * M],
+                in_=w_grp[:, c0:c1].rearrange("p c m j -> p (c m j)"),
+            )
+
+        def multiply(c, r0):
+            hi = r0 + dict(RANGES)[r0]
             nc.tensor.matmul_mx(
                 out=banks[r0][:],
                 lhsT=w_codes[:, c * M : (c + 1) * M].bitcast(FP8X4),
                 lhsT_scale=w_scales[:, c * M : (c + 1) * M],
-                rhs=part(x_codes, c, lo, hi).bitcast(FP8X4),
-                rhs_scale=part(x_scales, c, lo, hi),
+                rhs=part(x_codes, c, r0, hi).bitcast(FP8X4),
+                rhs_scale=part(x_scales, c, r0, hi),
                 start=(c == 0),
                 stop=(c == PASSES - 1),
             )
 
-        def bring(t0, n):
+        def bring(t0):
+            n = dict(RANGES)[t0]
             nc.scalar.activation(out=y[:, t0 : t0 + n], in_=banks[t0][:], func=IDENTITY, bias=bias[:])
 
-        def late_nodes(copy, t0, lo, hi):
-            interleave(copy, part(grp, 1, lo, hi), late[t0][:, :, lo - t0 : hi - t0])
+        def bring_vec(t0):
+            n = dict(RANGES)[t0]
+            nc.vector.tensor_scalar(out=y[:, t0 : t0 + n], in0=banks[t0][:], scalar1=bias[:], scalar2=None, op0=ADD)
+
+        def weave(copy, c, lo, hi, j=0):
+            c, j0, j1, t0, t1, raw = [r for r in raws if r[0] == c and r[1] == j and r[3] <= lo < r[4]][0]
+            interleave(copy, part(grp, c, lo, hi)[:, :, j0:j1], raw[:, :, lo - t0 : hi - t0])
+
+        def weave_w(copy, c):
+            interleave(copy, w_grp[:, c], w_raws[c])
 
         vec, sca = nc.vector.tensor_copy, nc.scalar.copy
-        interleave(vec, part(grp, 0, 0, 368), raw0[:, :, 0:368])
-        interleave(sca, part(grp, 0, 368, 512), raw0[:, :, 368:512])
-        interleave(sca, part(grp, 0, 512, 768), raw0[:, :, 512:768])
-        interleave(sca, part(grp, 0, 768, T), raw0[:, :, 768:T])
-        interleave(vec, w_grp[:, 0], w_raw[:, 0])
-        interleave(vec, w_grp[:, 1], w_raw[:, 1])
+        weave(vec, 0, 0, 368)
+        weave(sca, 0, 368, 512)
+        weave(sca, 0, 512, 768)
+        weave(sca, 0, 768, T)
+        weave_w(vec, 0)
+        weave_w(vec, 1)
         quantize(0, 0, 512)
-        nc.vector.quantize_mx(
-            out=w_codes[:].bitcast(FP8X4), scales=w_scales[:], in_=w_grp[:].rearrange("p c m j -> p (c m j)")
-        )
+        quantize_w(0, 2)
         quantize(0, 512, 256)
         quantize(0, 768, 256)
         for r0, rn in RANGES:
-            multiply(0, r0, r0, r0 + rn)
-        late_nodes(vec, 0, 0, 256)
-        late_nodes(sca, 0, 256, 512)
+            multiply(0, r0)
+        weave(vec, 1, 0, 256)
+        weave(sca, 1, 256, 512)
         quantize(1, 0, 256)
         quantize(1, 256, 256)
-        multiply(1, 0, 0, 512)
-        late_nodes(vec, 512, 512, 640)
-        late_nodes(sca, 512, 640, 768)
+        multiply(1, 0)
+        weave(vec, 1, 512, 640)
+        weave(sca, 1, 640, 768)
         quantize(1, 512, 256)
-        multiply(1, 512, 512, 768)
-        late_nodes(vec, 768, 768, 944)
-        late_nodes(sca, 768, 944, T)
+        multiply(1, 512)
+        weave(vec, 1, 768, 944)
+        weave(sca, 1, 944, T)
         quantize(1, 768, 256)
-        multiply(1, 768, 768, 896)
-        multiply(1, 896, 896, T)
-        for t0, n in RANGES[:3]:
-            bring(t0, n)
-        t0, n = RANGES[3]
-        nc.vector.tensor_scalar(out=y[:, t0 : t0 + n], in0=banks[t0][:], scalar1=bias[:], scalar2=None, op0=ADD)
+        multiply(1, 768)
+        multiply(1, 896)
+        bring(0)
+        bring(512)
+        bring_vec(768)
+        bring(896)
 
         prods = []
         accs = []

@@ -51,8 +51,7 @@ def tile_picked_agg_lin_bias_sub_l_kernel(
         def load_w(c0, c1):
             raw = keep.tile([P, c1 - c0, PACK, M], F32, name=f"w_raw{c0}")
             nc.sync.dma_start(out=raw[:], in_=w_rows[:, c0:c1])
-            for c in range(c0, c1):
-                w_raws[c] = raw[:, c - c0]
+            w_raws[c0] = raw[:]
 
         bias = keep.tile([P, 1], F32, name="bias")
         load_x(0, 0, 4, 0, T)
@@ -134,16 +133,18 @@ def tile_picked_agg_lin_bias_sub_l_kernel(
             c, j0, j1, t0, t1, raw = [r for r in raws if r[0] == c and r[1] == j and r[3] <= lo < r[4]][0]
             interleave(copy, part(grp, c, lo, hi)[:, :, j0:j1], raw[:, :, lo - t0 : hi - t0])
 
-        def weave_w(copy, c):
-            interleave(copy, w_grp[:, c], w_raws[c])
+        def weave_w(copy):
+            copy(
+                out=w_grp[:].rearrange("p c (g i) j -> p c g j i", i=2),
+                in_=w_raws[0].rearrange("p c j (g i) -> p c g j i", i=2),
+            )
 
         vec, sca = nc.vector.tensor_copy, nc.scalar.copy
         weave(vec, 0, 0, 368)
         weave(sca, 0, 368, 512)
         weave(sca, 0, 512, 768)
         weave(sca, 0, 768, T)
-        weave_w(vec, 0)
-        weave_w(vec, 1)
+        weave_w(vec)
         quantize(0, 0, 512)
         quantize_w(0, 2)
         quantize(0, 512, 256)
@@ -159,10 +160,11 @@ def tile_picked_agg_lin_bias_sub_l_kernel(
         weave(sca, 1, 640, 768)
         quantize(1, 512, 256)
         multiply(1, 512)
-        weave(vec, 1, 768, 944)
-        weave(sca, 1, 944, T)
-        quantize(1, 768, 256)
+        weave(vec, 1, 768, 896)
+        weave(sca, 1, 896, T)
+        quantize(1, 768, 128)
         multiply(1, 768)
+        quantize(1, 896, 128)
         multiply(1, 896)
         bring(0)
         bring(512)

@@ -133,27 +133,30 @@ def tile_picked_agg_lin_bias_sub_l_kernel(
             c, j0, j1, t0, t1, raw = [r for r in raws if r[0] == c and r[1] == j and r[3] <= lo < r[4]][0]
             interleave(copy, part(grp, c, lo, hi)[:, :, j0:j1], raw[:, :, lo - t0 : hi - t0])
 
-        def weave_w(copy):
-            copy(
-                out=w_grp[:].rearrange("p c (g i) j -> p c g j i", i=2),
-                in_=w_raws[0].rearrange("p c j (g i) -> p c g j i", i=2),
-            )
+        def weave_w(copy, c):
+            interleave(copy, w_grp[:, c], w_raws[0][:, c])
 
         vec, sca = nc.vector.tensor_copy, nc.scalar.copy
-        weave(vec, 0, 0, 368)
+        weave(vec, 0, 0, 256)
+        weave(vec, 0, 256, 368)
         weave(sca, 0, 368, 512)
         weave(sca, 0, 512, 768)
         weave(sca, 0, 768, T)
-        weave_w(vec)
-        quantize(0, 0, 512)
-        quantize_w(0, 2)
+        weave_w(vec, 0)
+        weave_w(vec, 1)
+        quantize(0, 0, 256)
+        quantize(0, 256, 256)
+        quantize_w(0, 1)
+        quantize_w(1, 2)
         quantize(0, 512, 256)
         quantize(0, 768, 256)
         for r0, rn in RANGES:
             multiply(0, r0)
-        weave(vec, 1, 0, 256)
+        weave(vec, 1, 0, 128)
+        weave(vec, 1, 128, 256)
         weave(sca, 1, 256, 512)
-        quantize(1, 0, 256)
+        quantize(1, 0, 128)
+        quantize(1, 128, 128)
         quantize(1, 256, 256)
         multiply(1, 0)
         weave(vec, 1, 512, 640)
@@ -179,7 +182,7 @@ def tile_picked_agg_lin_bias_sub_l_kernel(
         for i in range(V // P):
             acc = psum.tile([P, P], F32, name=f"acc{i}")
             accs.append(acc)
-        backs = [psum.tile([P, 2 * P], F32, name=f"back{h}", tag=("y0", "y512")[h]) for h in range(2)]
+        backs = [psum.tile([P, n], F32, name=f"back{h}", tag=("y0", "y512", "y768")[h]) for h, n in enumerate((2 * P, P, P))]
         turned = keep.tile([P, V], F32, name="turned")
         res = keep.tile([P, V], F32, name="res")
 
@@ -197,17 +200,18 @@ def tile_picked_agg_lin_bias_sub_l_kernel(
             gather(d, 0, V)
             for i in range(4):
                 add_up(d, i, D - 2)
-        for h in range(2):
-            gather(D - 2, 2 * h * P, 2 * (h + 1) * P)
-            for i in (2 * h, 2 * h + 1):
+        for blocks in ((0, 1), (2,), (3,)):
+            gather(D - 2, blocks[0] * P, (blocks[-1] + 1) * P)
+            for i in blocks:
                 add_up(D - 2, i, D - 2)
         for i in range(4):
             nc.scalar.copy(out=turned[:, i * P : (i + 1) * P], in_=accs[i][:])
         for i in range(4):
-            nc.tensor.transpose(backs[i // 2][:, i % 2 * P : (i % 2 + 1) * P], turned[:, i * P : (i + 1) * P], ident[:])
-        for h in range(2):
-            gather(D - 1, 2 * h * P, 2 * (h + 1) * P)
-        for h in range(2):
-            lo, hi = 2 * h * P, 2 * (h + 1) * P
-            nc.vector.tensor_tensor(res[:, lo:hi], prods[7][:, lo:hi], backs[h][:], ADD)
-            nc.sync.dma_start(out=out[:, lo:hi], in_=res[:, lo:hi])
+            back = backs[0][:, i * P : (i + 1) * P] if i < 2 else backs[i - 1][:]
+            nc.tensor.transpose(back, turned[:, i * P : (i + 1) * P], ident[:])
+        gather(D - 1, 0, 3 * P)
+        gather(D - 1, 3 * P, V)
+        for lo, hi, bank in ((0, 2 * P, 0), (2 * P, 3 * P, 1), (3 * P, V, 2)):
+            nc.vector.tensor_tensor(res[:, lo:hi], prods[7][:, lo:hi], backs[bank][:], ADD)
+            if hi % (2 * P) == 0:
+                nc.sync.dma_start(out=out[:, hi - 2 * P : hi], in_=res[:, hi - 2 * P : hi])

@@ -22,8 +22,9 @@ ADD = mybir.AluOpType.add
 IDENTITY = mybir.ActivationFunctionType.Identity
 
 
-RANGES = ((0, 512), (512, 256), (768, 128), (896, 128))
-UNITS = ((0, 0, 512), (0, 512, 512), (1, 0, 512), (1, 512, 256), (1, 768, 256))
+GATE_LOADS = ((0, 1), (1, 2), (2, 3), (3, 4), (4, 5), (5, 6), (6, 8))
+RANGES = ((0, 256), (256, 128), (384, 256), (640, 128), (768, 128), (896, 128))
+UNITS = ((0, 0, 384), (0, 384, 256), (0, 640, 384), (1, 0, 384), (1, 384, 256), (1, 640, 256), (1, 896, 128))
 
 
 def tile_picked_agg_lin_bias_sub_l_kernel(
@@ -41,34 +42,39 @@ def tile_picked_agg_lin_bias_sub_l_kernel(
         x_rows = xT.rearrange("(c p j) t -> c p j t", c=PASSES, j=PACK)
         w_rows = w.rearrange("(c p j) m -> p c j m", c=PASSES, j=PACK)
         raws = []
-        w_raws = {}
 
-        def load_x(c, j0, j1, t0, t1, tag=None):
-            raw = keep.tile([P, j1 - j0, t1 - t0], F32, name=f"raw{c}_{j0}_{t0}", tag=tag or f"raw{c}_{j0}_{t0}")
+        def load_x(c, j0, j1, t0, t1):
+            raw = keep.tile([P, j1 - j0, t1 - t0], F32, name=f"raw{c}_{j0}_{t0}")
             nc.sync.dma_start(out=raw[:], in_=x_rows[c][:, j0:j1, t0:t1])
             raws.append((c, j0, j1, t0, t1, raw))
 
-        def load_w(c0, c1):
-            raw = keep.tile([P, c1 - c0, PACK, M], F32, name=f"w_raw{c0}")
-            nc.sync.dma_start(out=raw[:], in_=w_rows[:, c0:c1])
-            w_raws[c0] = raw[:]
-
+        w_raw = keep.tile([P, PASSES, PACK, M], F32, name="w_raw")
         bias = keep.tile([P, 1], F32, name="bias")
+
+        def load_w():
+            nc.sync.dma_start(out=w_raw[:], in_=w_rows)
+
+        def load_bias():
+            nc.sync.dma_start(out=bias[:], in_=b)
+
         load_x(0, 0, 4, 0, T)
-        load_w(0, 2)
-        load_x(1, 0, 4, 0, 512)
-        load_x(1, 0, 4, 512, 768)
-        load_x(1, 0, 4, 768, T)
-        nc.sync.dma_start(out=bias[:], in_=b)
+        load_w()
+        load_x(1, 0, 4, 0, 384)
+        load_x(1, 0, 4, 384, 640)
+        load_x(1, 0, 4, 640, 896)
+        load_x(1, 0, 4, 896, T)
+        load_bias()
         offs = []
         gates = []
         for d in range(D):
             off = keep.tile([P, V // 16], U16, name=f"off{d}")
             nc.sync.dma_start(off[:], lists[d])
             offs.append(off)
-            g = keep.tile([P, V], F32, name=f"gate{d}")
-            nc.sync.dma_start(out=g[:], in_=gate[d])
-            gates.append(g)
+            for d0, d1 in GATE_LOADS:
+                if d0 == d:
+                    g = keep.tile([P, d1 - d0, V], F32, name=f"gate{d}")
+                    nc.sync.dma_start(out=g[:], in_=gate[d0:d1].rearrange("d p v -> p d v"))
+                    gates.extend(g[:, i, :] for i in range(d1 - d0))
 
         def interleave(copy, grouped, raw):
             copy(
@@ -91,9 +97,8 @@ def tile_picked_agg_lin_bias_sub_l_kernel(
             return tiles[c, t0][:, lo - t0 : hi - t0]
 
         banks = {}
-        for t0, n in RANGES:
-            bank = psum.tile([P, n], F32, name=f"y{t0}")
-            banks[t0] = bank
+        for i, (t0, n) in enumerate(RANGES):
+            banks[t0] = psum.tile([P, n], F32, name=f"y{t0}", tag=f"bank{i}")
 
         def quantize(c, t0, n):
             nc.vector.quantize_mx(
@@ -133,56 +138,62 @@ def tile_picked_agg_lin_bias_sub_l_kernel(
             c, j0, j1, t0, t1, raw = [r for r in raws if r[0] == c and r[1] == j and r[3] <= lo < r[4]][0]
             interleave(copy, part(grp, c, lo, hi)[:, :, j0:j1], raw[:, :, lo - t0 : hi - t0])
 
-        def weave_w(copy, c):
-            interleave(copy, w_grp[:, c], w_raws[0][:, c])
+        def weave_w(copy, c0, c1):
+            copy(
+                out=w_grp[:, c0:c1].rearrange("p c (g i) j -> p c g j i", i=2),
+                in_=w_raw[:, c0:c1].rearrange("p c j (g i) -> p c g j i", i=2),
+            )
 
         vec, sca = nc.vector.tensor_copy, nc.scalar.copy
-        weave(vec, 0, 0, 256)
-        weave(vec, 0, 256, 368)
-        weave(sca, 0, 368, 512)
-        weave(sca, 0, 512, 768)
-        weave(sca, 0, 768, T)
-        weave_w(vec, 0)
-        weave_w(vec, 1)
+        weave(vec, 0, 0, 384)
+        weave(sca, 0, 384, 640)
+        weave(sca, 0, 640, 896)
+        weave(vec, 0, 896, T)
         quantize(0, 0, 256)
-        quantize(0, 256, 256)
+        quantize(0, 256, 128)
+        weave_w(vec, 0, 1)
+        weave_w(sca, 1, 2)
+        quantize(0, 384, 256)
         quantize_w(0, 1)
+        quantize(0, 896, 128)
+        quantize(0, 640, 256)
         quantize_w(1, 2)
-        quantize(0, 512, 256)
-        quantize(0, 768, 256)
         for r0, rn in RANGES:
             multiply(0, r0)
         weave(vec, 1, 0, 128)
-        weave(vec, 1, 128, 256)
-        weave(sca, 1, 256, 512)
+        weave(vec, 1, 128, 192)
+        weave(sca, 1, 192, 256)
+        weave(sca, 1, 256, 384)
         quantize(1, 0, 128)
         quantize(1, 128, 128)
-        quantize(1, 256, 256)
+        quantize(1, 256, 128)
         multiply(1, 0)
-        weave(vec, 1, 512, 640)
-        weave(sca, 1, 640, 768)
-        quantize(1, 512, 256)
-        multiply(1, 512)
-        weave(vec, 1, 768, 896)
-        weave(sca, 1, 896, T)
+        multiply(1, 256)
+        weave(vec, 1, 384, 512)
+        weave(vec, 1, 512, 544)
+        weave(sca, 1, 544, 640)
+        quantize(1, 384, 128)
+        quantize(1, 512, 128)
+        multiply(1, 384)
+        weave(vec, 1, 640, 768)
+        weave(sca, 1, 768, 896)
+        weave(vec, 1, 896, T)
+        quantize(1, 640, 128)
+        multiply(1, 640)
         quantize(1, 768, 128)
         multiply(1, 768)
         quantize(1, 896, 128)
         multiply(1, 896)
         bring(0)
-        bring(512)
+        bring(256)
+        bring(384)
+        bring(640)
         bring_vec(768)
         bring(896)
 
-        prods = []
-        accs = []
-        for d in range(D):
-            prod = keep.tile([P, V], F32, name=f"prod{d}")
-            prods.append(prod)
-        for i in range(V // P):
-            acc = psum.tile([P, P], F32, name=f"acc{i}")
-            accs.append(acc)
-        backs = [psum.tile([P, n], F32, name=f"back{h}", tag=("y0", "y512", "y768")[h]) for h, n in enumerate((2 * P, P, P))]
+        prods = [keep.tile([P, V], F32, name=f"prod{d}") for d in range(D)]
+        accs = [psum.tile([P, P], F32, name=f"acc{i}", tag=f"bank{(6 + i) % 8}") for i in range(V // P)]
+        backs = [psum.tile([P, n], F32, name=f"back{h}", tag=f"bank{2 + h}") for h, n in enumerate((2 * P, P, P))]
         turned = keep.tile([P, V], F32, name="turned")
         res = keep.tile([P, V], F32, name="res")
 

@@ -185,9 +185,9 @@ def tile_picked_agg_lin_bias_sub_l_kernel(
         quantize(1, 896, 128)
         multiply(1, 896)
         bring(0)
-        bring(256)
         bring(384)
-        bring(640)
+        bring_vec(256)
+        bring_vec(640)
         bring_vec(768)
         bring(896)
 

@@ -22,7 +22,6 @@ ADD = mybir.AluOpType.add
 IDENTITY = mybir.ActivationFunctionType.Identity
 
 
-GATE_LOADS = ((0, 1), (1, 2), (2, 3), (3, 4), (4, 5), (5, 6), (6, 8))
 RANGES = ((0, 256), (256, 128), (384, 256), (640, 128), (768, 128), (896, 128))
 UNITS = ((0, 0, 384), (0, 384, 256), (0, 640, 384), (1, 0, 384), (1, 384, 256), (1, 640, 256), (1, 896, 128))
 
@@ -59,8 +58,7 @@ def tile_picked_agg_lin_bias_sub_l_kernel(
 
         load_x(0, 0, 4, 0, T)
         load_w()
-        load_x(1, 0, 4, 0, 384)
-        load_x(1, 0, 4, 384, 640)
+        load_x(1, 0, 4, 0, 640)
         load_x(1, 0, 4, 640, 896)
         load_x(1, 0, 4, 896, T)
         load_bias()
@@ -70,11 +68,9 @@ def tile_picked_agg_lin_bias_sub_l_kernel(
             off = keep.tile([P, V // 16], U16, name=f"off{d}")
             nc.sync.dma_start(off[:], lists[d])
             offs.append(off)
-            for d0, d1 in GATE_LOADS:
-                if d0 == d:
-                    g = keep.tile([P, d1 - d0, V], F32, name=f"gate{d}")
-                    nc.sync.dma_start(out=g[:], in_=gate[d0:d1].rearrange("d p v -> p d v"))
-                    gates.extend(g[:, i, :] for i in range(d1 - d0))
+            g = keep.tile([P, V], F32, name=f"gate{d}")
+            nc.sync.dma_start(out=g[:], in_=gate[d])
+            gates.append(g)
 
         def interleave(copy, grouped, raw):
             copy(
@@ -160,20 +156,15 @@ def tile_picked_agg_lin_bias_sub_l_kernel(
         quantize_w(1, 2)
         for r0, rn in RANGES:
             multiply(0, r0)
-        weave(vec, 1, 0, 128)
-        weave(vec, 1, 128, 192)
-        weave(sca, 1, 192, 256)
+        weave(vec, 1, 0, 256)
+        weave(vec, 1, 384, 480)
         weave(sca, 1, 256, 384)
-        quantize(1, 0, 128)
-        quantize(1, 128, 128)
+        weave(sca, 1, 480, 640)
+        quantize(1, 0, 256)
         quantize(1, 256, 128)
         multiply(1, 0)
         multiply(1, 256)
-        weave(vec, 1, 384, 512)
-        weave(vec, 1, 512, 544)
-        weave(sca, 1, 544, 640)
-        quantize(1, 384, 128)
-        quantize(1, 512, 128)
+        quantize(1, 384, 256)
         multiply(1, 384)
         weave(vec, 1, 640, 768)
         weave(sca, 1, 768, 896)

@@ -20,9 +20,11 @@ FP8X4 = mybir.dt.float8_e4m3fn_x4
 MULT = mybir.AluOpType.mult
 ADD = mybir.AluOpType.add
 IDENTITY = mybir.ActivationFunctionType.Identity
+COPY = mybir.ActivationFunctionType.Copy
 
 
 RANGES = ((0, 256), (256, 128), (384, 256), (640, 128), (768, 128), (896, 128))
+ENDS = ((256, 512), (0, 128), (128, 256))
 UNITS = ((0, 0, 384), (0, 384, 256), (0, 640, 384), (1, 0, 384), (1, 384, 256), (1, 640, 256), (1, 896, 128))
 
 
@@ -62,15 +64,37 @@ def tile_picked_agg_lin_bias_sub_l_kernel(
         load_x(1, 0, 4, 640, 896)
         load_x(1, 0, 4, 896, T)
         load_bias()
-        offs = []
-        gates = []
-        for d in range(D):
-            off = keep.tile([P, V // 16], U16, name=f"off{d}")
-            nc.sync.dma_start(off[:], lists[d])
-            offs.append(off)
-            g = keep.tile([P, V], F32, name=f"gate{d}")
-            nc.sync.dma_start(out=g[:], in_=gate[d])
-            gates.append(g)
+        offs = [keep.tile([P, V // 16], U16, name=f"off{d}") for d in range(D)]
+        gate_parts = []
+
+        def load_list(d):
+            nc.sync.dma_start(offs[d][:], lists[d])
+
+        def load_gate(d0, d1, lo=0, hi=V):
+            g = keep.tile([P, d1 - d0, hi - lo], F32, name=f"gate{d0}_{lo}")
+            nc.sync.dma_start(out=g[:], in_=gate[d0:d1, :, lo:hi].rearrange("d p v -> p d v"))
+            gate_parts.append((d0, d1, lo, hi, g))
+
+        def gate_of(d, lo, hi):
+            d0, d1, v0, v1, g = [e for e in gate_parts if e[0] <= d < e[1] and e[2] <= lo < e[3]][0]
+            return g[:, d - d0, lo - v0 : hi - v0]
+
+        load_list(0)
+        load_list(1)
+        load_gate(0, 1)
+        load_list(3)
+        load_gate(1, 2)
+        load_list(2)
+        load_gate(2, 3)
+        load_list(4)
+        load_gate(3, 5)
+        load_list(5)
+        load_list(6)
+        load_gate(6, 7, 256, 512)
+        load_gate(5, 6)
+        load_gate(6, 7, 0, 256)
+        load_list(7)
+        load_gate(7, 8)
 
         def interleave(copy, grouped, raw):
             copy(
@@ -183,37 +207,73 @@ def tile_picked_agg_lin_bias_sub_l_kernel(
         bring(896)
 
         prods = [keep.tile([P, V], F32, name=f"prod{d}") for d in range(D)]
+        picked = [keep.tile([P, V], F32, name=f"picked{d}") for d in range(D)]
         accs = [psum.tile([P, P], F32, name=f"acc{i}", tag=f"bank{(6 + i) % 8}") for i in range(V // P)]
-        backs = [psum.tile([P, n], F32, name=f"back{h}", tag=f"bank{2 + h}") for h, n in enumerate((2 * P, P, P))]
+        backs = {lo: psum.tile([P, hi - lo], F32, name=f"back{lo}", tag=f"bank{2 + h}") for h, (lo, hi) in enumerate(ENDS)}
         turned = keep.tile([P, V], F32, name="turned")
         res = keep.tile([P, V], F32, name="res")
 
-        def gather(d, lo, hi):
+        def fused(d, lo=0, hi=V):
             nc.vector.tensor_tensor(
-                prods[d][:, lo:hi], y[:].indirect(offs[d][:, lo // 16 : hi // 16]), gates[d][:, lo:hi], MULT
+                prods[d][:, lo:hi], y[:].indirect(offs[d][:, lo // 16 : hi // 16]), gate_of(d, lo, hi), MULT
             )
 
-        def add_up(d, i, last):
-            nc.tensor.matmul(
-                accs[i][:], prods[d][:, i * P : (i + 1) * P], ident[:], start=(d == 0), stop=(d == last), is_transpose=True
-            )
+        def pick(d, lo=0, hi=V):
+            nc.scalar.activation(picked[d][:, lo:hi], y[:].indirect(offs[d][:, lo // 16 : hi // 16]), COPY)
 
-        for d in range(D - 2):
-            gather(d, 0, V)
-            for i in range(4):
-                add_up(d, i, D - 2)
-        for blocks in ((0, 1), (2,), (3,)):
-            gather(D - 2, blocks[0] * P, (blocks[-1] + 1) * P)
-            for i in blocks:
-                add_up(D - 2, i, D - 2)
-        for i in range(4):
-            nc.scalar.copy(out=turned[:, i * P : (i + 1) * P], in_=accs[i][:])
-        for i in range(4):
-            back = backs[0][:, i * P : (i + 1) * P] if i < 2 else backs[i - 1][:]
-            nc.tensor.transpose(back, turned[:, i * P : (i + 1) * P], ident[:])
-        gather(D - 1, 0, 3 * P)
-        gather(D - 1, 3 * P, V)
-        for lo, hi, bank in ((0, 2 * P, 0), (2 * P, 3 * P, 1), (3 * P, V, 2)):
-            nc.vector.tensor_tensor(res[:, lo:hi], prods[7][:, lo:hi], backs[bank][:], ADD)
-            if hi % (2 * P) == 0:
-                nc.sync.dma_start(out=out[:, hi - 2 * P : hi], in_=res[:, hi - 2 * P : hi])
+        def weigh(d, lo=0, hi=V):
+            nc.vector.tensor_tensor(prods[d][:, lo:hi], picked[d][:, lo:hi], gate_of(d, lo, hi), MULT)
+
+        def add_up(d, lo=0, hi=V, last=False):
+            for i in range(lo // P, hi // P):
+                nc.tensor.matmul(
+                    accs[i][:], prods[d][:, i * P : (i + 1) * P], ident[:], start=(d == 0), stop=last, is_transpose=True
+                )
+
+        def turn_back(lo, hi):
+            for v in range(lo, hi, P):
+                nc.scalar.copy(out=turned[:, v : v + P], in_=accs[v // P][:])
+            for v in range(lo, hi, P):
+                nc.tensor.transpose(backs[lo][:, v - lo : v - lo + P], turned[:, v : v + P], ident[:])
+
+        def finish(lo, hi):
+            nc.vector.tensor_tensor(res[:, lo:hi], prods[D - 1][:, lo:hi], backs[lo][:], ADD)
+
+        def store(lo, hi):
+            nc.sync.dma_start(out=out[:, lo:hi], in_=res[:, lo:hi])
+
+        pick(1)
+        pick(3)
+        pick(4)
+        pick(5)
+        pick(6, 0, 128)
+        pick(6, 128, 256)
+        fused(0)
+        add_up(0)
+        weigh(1)
+        add_up(1)
+        fused(2)
+        add_up(2)
+        weigh(3)
+        add_up(3)
+        weigh(4)
+        add_up(4)
+        fused(6, 256, 512)
+        add_up(6, 256, 512)
+        weigh(5)
+        add_up(5, 256, 512, last=True)
+        add_up(5, 0, 256)
+        weigh(6, 0, 128)
+        add_up(6, 0, 128, last=True)
+        weigh(6, 128, 256)
+        add_up(6, 128, 256, last=True)
+        turn_back(256, 512)
+        turn_back(0, 128)
+        turn_back(128, 256)
+        fused(7, 256, 512)
+        fused(7, 0, 256)
+        finish(256, 512)
+        store(256, 512)
+        finish(0, 128)
+        finish(128, 256)
+        store(0, 256)

@@ -87,12 +87,11 @@ def tile_picked_agg_lin_bias_sub_l_kernel(
         load_list(2)
         load_gate(2, 3)
         load_list(4)
-        load_gate(3, 5)
+        load_gate(3, 4)
+        load_gate(4, 5)
         load_list(5)
         load_list(6)
-        load_gate(6, 7, 256, 512)
-        load_gate(5, 6)
-        load_gate(6, 7, 0, 256)
+        load_gate(5, 7)
         load_list(7)
         load_gate(7, 8)
 
@@ -245,7 +244,8 @@ def tile_picked_agg_lin_bias_sub_l_kernel(
         pick(1)
         pick(3)
         pick(4)
-        pick(5)
+        pick(5, 256, 512)
+        pick(5, 0, 256)
         pick(6, 0, 128)
         pick(6, 128, 256)
         fused(0)
@@ -260,8 +260,9 @@ def tile_picked_agg_lin_bias_sub_l_kernel(
         add_up(4)
         fused(6, 256, 512)
         add_up(6, 256, 512)
-        weigh(5)
+        weigh(5, 256, 512)
         add_up(5, 256, 512, last=True)
+        weigh(5, 0, 256)
         add_up(5, 0, 256)
         weigh(6, 0, 128)
         add_up(6, 0, 128, last=True)
@@ -275,5 +276,6 @@ def tile_picked_agg_lin_bias_sub_l_kernel(
         finish(256, 512)
         store(256, 512)
         finish(0, 128)
+        store(0, 128)
         finish(128, 256)
-        store(0, 256)
+        store(128, 256)

@@ -269,10 +269,12 @@ def tile_picked_agg_lin_bias_sub_l_kernel(
         weigh(6, 128, 256)
         add_up(6, 128, 256, last=True)
         turn_back(256, 512)
+        pick(7, 128, 256)
         turn_back(0, 128)
         turn_back(128, 256)
         fused(7, 256, 512)
-        fused(7, 0, 256)
+        fused(7, 0, 128)
+        weigh(7, 128, 256)
         finish(256, 512)
         store(256, 512)
         finish(0, 128)

@@ -24,7 +24,7 @@ COPY = mybir.ActivationFunctionType.Copy
 
 
 RANGES = ((0, 256), (256, 128), (384, 256), (640, 128), (768, 128), (896, 128))
-ENDS = ((256, 512), (0, 128), (128, 256))
+ENDS = ((256, 512), (128, 256), (0, 128))
 UNITS = ((0, 0, 384), (0, 384, 256), (0, 640, 384), (1, 0, 384), (1, 384, 256), (1, 640, 256), (1, 896, 128))
 
 
@@ -88,12 +88,12 @@ def tile_picked_agg_lin_bias_sub_l_kernel(
         load_gate(2, 3)
         load_list(4)
         load_gate(3, 4)
-        load_gate(4, 5)
         load_list(5)
         load_list(6)
-        load_gate(5, 7)
+        load_gate(4, 7)
         load_list(7)
-        load_gate(7, 8)
+        load_gate(7, 8, 256, 512)
+        load_gate(7, 8, 0, 256)
 
         def interleave(copy, grouped, raw):
             copy(
@@ -200,7 +200,7 @@ def tile_picked_agg_lin_bias_sub_l_kernel(
         multiply(1, 896)
         bring(0)
         bring(384)
-        bring_vec(256)
+        bring(256)
         bring_vec(640)
         bring_vec(768)
         bring(896)
@@ -241,43 +241,49 @@ def tile_picked_agg_lin_bias_sub_l_kernel(
         def store(lo, hi):
             nc.sync.dma_start(out=out[:, lo:hi], in_=res[:, lo:hi])
 
-        pick(1)
+        pick(1, 256, 512)
+        pick(1, 0, 256)
         pick(3)
         pick(4)
         pick(5, 256, 512)
         pick(5, 0, 256)
         pick(6, 0, 128)
-        pick(6, 128, 256)
         fused(0)
         add_up(0)
-        weigh(1)
-        add_up(1)
-        fused(2)
-        add_up(2)
+        weigh(1, 256, 512)
+        add_up(1, 256, 512)
+        weigh(1, 0, 256)
+        add_up(1, 0, 256)
+        fused(2, 256, 512)
+        add_up(2, 256, 512)
+        fused(2, 0, 256)
+        add_up(2, 0, 256)
         weigh(3)
         add_up(3)
-        weigh(4)
-        add_up(4)
         fused(6, 256, 512)
         add_up(6, 256, 512)
+        weigh(4, 256, 512)
+        add_up(4, 256, 512)
         weigh(5, 256, 512)
         add_up(5, 256, 512, last=True)
+        fused(6, 128, 256)
+        add_up(6, 128, 256)
+        weigh(4, 0, 256)
+        add_up(4, 0, 256)
         weigh(5, 0, 256)
-        add_up(5, 0, 256)
+        add_up(5, 128, 256, last=True)
+        add_up(5, 0, 128)
         weigh(6, 0, 128)
         add_up(6, 0, 128, last=True)
-        weigh(6, 128, 256)
-        add_up(6, 128, 256, last=True)
+        pick(7, 0, 256)
         turn_back(256, 512)
-        pick(7, 128, 256)
-        turn_back(0, 128)
         turn_back(128, 256)
+        turn_back(0, 128)
         fused(7, 256, 512)
-        fused(7, 0, 128)
-        weigh(7, 128, 256)
         finish(256, 512)
         store(256, 512)
-        finish(0, 128)
-        store(0, 128)
+        weigh(7, 0, 256)
         finish(128, 256)
         store(128, 256)
+        finish(0, 128)
+        store(0, 128)

@@ -23,7 +23,11 @@ IDENTITY = mybir.ActivationFunctionType.Identity
 COPY = mybir.ActivationFunctionType.Copy
 
 
+BANKS = ((0, 384), (384, 256), (640, 128), (768, 128), (896, 128))
 RANGES = ((0, 256), (256, 128), (384, 256), (640, 128), (768, 128), (896, 128))
+BLOCKS = V // P
+SPREAD = range(2, 14)
+ROW_STEP = 32 * V + P
 ENDS = ((256, 512), (128, 256), (0, 128))
 UNITS = ((0, 0, 384), (0, 384, 256), (0, 640, 384), (1, 0, 384), (1, 384, 256), (1, 640, 256), (1, 896, 128))
 
@@ -59,6 +63,21 @@ def tile_picked_agg_lin_bias_sub_l_kernel(
             nc.sync.dma_start(out=bias[:], in_=b)
 
         load_x(0, 0, 4, 0, T)
+        gate_rows = keep.tile([P, P], F32, name="gate_rows")
+        nc.vector.memset(gate_rows[:], 0.0)
+        n_rows = len(SPREAD)
+        flat = gate.rearrange("d p v -> (d p v)")[SPREAD[0] * ROW_STEP : (SPREAD[-1] + 1) * ROW_STEP]
+        nc.sync.dma_start(out=gate_rows[0:n_rows, :], in_=flat.rearrange("(i c) -> i c", c=ROW_STEP)[:, 0:P])
+        rows_turned = psum.tile([P, P], F32, name="rows_turned", tag="bank4")
+        nc.tensor.transpose(rows_turned[:], gate_rows[:], ident[:])
+        gate_cols = keep.tile([P, n_rows], F32, name="gate_cols")
+        nc.scalar.copy(out=gate_cols[:], in_=rows_turned[:, 0:n_rows])
+        spread = [psum.tile([P, V], F32, name=f"spread{n}", tag=f"bank{5 + n}") for n in range(n_rows // BLOCKS)]
+        for n, row in enumerate(SPREAD):
+            d, i = divmod(row, BLOCKS)
+            col = gate_cols[:, n : n + 1]
+            nc.tensor.transpose(spread[d % 3][:, i * P : (i + 1) * P], col.to_broadcast([P, P]), ident[:])
+
         load_w()
         load_x(1, 0, 4, 0, 640)
         load_x(1, 0, 4, 640, 896)
@@ -76,24 +95,25 @@ def tile_picked_agg_lin_bias_sub_l_kernel(
             gate_parts.append((d0, d1, lo, hi, g))
 
         def gate_of(d, lo, hi):
+            if d * BLOCKS + lo // P in SPREAD:
+                return spread[d % 3][:, lo:hi]
             d0, d1, v0, v1, g = [e for e in gate_parts if e[0] <= d < e[1] and e[2] <= lo < e[3]][0]
             return g[:, d - d0, lo - v0 : hi - v0]
 
-        load_list(0)
-        load_list(1)
-        load_gate(0, 1)
-        load_list(3)
-        load_gate(1, 2)
-        load_list(2)
-        load_gate(2, 3)
         load_list(4)
-        load_gate(3, 4)
+        load_gate(4, 5)
         load_list(5)
+        load_gate(5, 6)
+        load_list(1)
+        load_list(3)
+        load_gate(3, 4, 256, 512)
         load_list(6)
-        load_gate(4, 7)
+        load_gate(6, 7)
+        load_list(0)
+        load_gate(0, 1, 0, 256)
+        load_list(2)
         load_list(7)
-        load_gate(7, 8, 256, 512)
-        load_gate(7, 8, 0, 256)
+        load_gate(7, 8)
 
         def interleave(copy, grouped, raw):
             copy(
@@ -116,7 +136,7 @@ def tile_picked_agg_lin_bias_sub_l_kernel(
             return tiles[c, t0][:, lo - t0 : hi - t0]
 
         banks = {}
-        for i, (t0, n) in enumerate(RANGES):
+        for i, (t0, n) in enumerate(BANKS):
             banks[t0] = psum.tile([P, n], F32, name=f"y{t0}", tag=f"bank{i}")
 
         def quantize(c, t0, n):
@@ -135,22 +155,23 @@ def tile_picked_agg_lin_bias_sub_l_kernel(
 
         def multiply(c, r0):
             hi = r0 + dict(RANGES)[r0]
+            t0, n = [e for e in BANKS if e[0] <= r0 < e[0] + e[1]][0]
             nc.tensor.matmul_mx(
-                out=banks[r0][:],
+                out=banks[t0][:, r0 - t0 : hi - t0],
                 lhsT=w_codes[:, c * M : (c + 1) * M].bitcast(FP8X4),
                 lhsT_scale=w_scales[:, c * M : (c + 1) * M],
                 rhs=part(x_codes, c, r0, hi).bitcast(FP8X4),
                 rhs_scale=part(x_scales, c, r0, hi),
-                start=(c == 0),
-                stop=(c == PASSES - 1),
+                start=(c == 0 and r0 == t0),
+                stop=(c == PASSES - 1 and hi == t0 + n),
             )
 
         def bring(t0):
-            n = dict(RANGES)[t0]
+            n = dict(BANKS)[t0]
             nc.scalar.activation(out=y[:, t0 : t0 + n], in_=banks[t0][:], func=IDENTITY, bias=bias[:])
 
         def bring_vec(t0):
-            n = dict(RANGES)[t0]
+            n = dict(BANKS)[t0]
             nc.vector.tensor_scalar(out=y[:, t0 : t0 + n], in0=banks[t0][:], scalar1=bias[:], scalar2=None, op0=ADD)
 
         def weave(copy, c, lo, hi, j=0):
@@ -200,15 +221,14 @@ def tile_picked_agg_lin_bias_sub_l_kernel(
         multiply(1, 896)
         bring(0)
         bring(384)
-        bring(256)
         bring_vec(640)
         bring_vec(768)
         bring(896)
 
         prods = [keep.tile([P, V], F32, name=f"prod{d}") for d in range(D)]
         picked = [keep.tile([P, V], F32, name=f"picked{d}") for d in range(D)]
-        accs = [psum.tile([P, P], F32, name=f"acc{i}", tag=f"bank{(6 + i) % 8}") for i in range(V // P)]
-        backs = {lo: psum.tile([P, hi - lo], F32, name=f"back{lo}", tag=f"bank{2 + h}") for h, (lo, hi) in enumerate(ENDS)}
+        accs = [psum.tile([P, P], F32, name=f"acc{i}", tag=f"bank{i}") for i in range(V // P)]
+        backs = {lo: psum.tile([P, hi - lo], F32, name=f"back{lo}", tag=f"bank{4 + h}") for h, (lo, hi) in enumerate(ENDS)}
         turned = keep.tile([P, V], F32, name="turned")
         res = keep.tile([P, V], F32, name="res")
 
@@ -223,10 +243,13 @@ def tile_picked_agg_lin_bias_sub_l_kernel(
         def weigh(d, lo=0, hi=V):
             nc.vector.tensor_tensor(prods[d][:, lo:hi], picked[d][:, lo:hi], gate_of(d, lo, hi), MULT)
 
+        def weigh_pool(d, lo, hi):
+            nc.gpsimd.tensor_tensor(prods[d][:, lo:hi], picked[d][:, lo:hi], gate_of(d, lo, hi), MULT)
+
         def add_up(d, lo=0, hi=V, last=False):
             for i in range(lo // P, hi // P):
                 nc.tensor.matmul(
-                    accs[i][:], prods[d][:, i * P : (i + 1) * P], ident[:], start=(d == 0), stop=last, is_transpose=True
+                    accs[i][:], prods[d][:, i * P : (i + 1) * P], ident[:], start=(d == 4), stop=last, is_transpose=True
                 )
 
         def turn_back(lo, hi):
@@ -241,48 +264,41 @@ def tile_picked_agg_lin_bias_sub_l_kernel(
         def store(lo, hi):
             nc.sync.dma_start(out=out[:, lo:hi], in_=res[:, lo:hi])
 
-        pick(1, 256, 512)
-        pick(1, 0, 256)
-        pick(3)
-        pick(4)
-        pick(5, 256, 512)
-        pick(5, 0, 256)
-        pick(6, 0, 128)
-        fused(0)
-        add_up(0)
-        weigh(1, 256, 512)
-        add_up(1, 256, 512)
-        weigh(1, 0, 256)
-        add_up(1, 0, 256)
-        fused(2, 256, 512)
-        add_up(2, 256, 512)
-        fused(2, 0, 256)
-        add_up(2, 0, 256)
-        weigh(3)
-        add_up(3)
-        fused(6, 256, 512)
-        add_up(6, 256, 512)
-        weigh(4, 256, 512)
-        add_up(4, 256, 512)
-        weigh(5, 256, 512)
-        add_up(5, 256, 512, last=True)
-        fused(6, 128, 256)
-        add_up(6, 128, 256)
-        weigh(4, 0, 256)
-        add_up(4, 0, 256)
-        weigh(5, 0, 256)
-        add_up(5, 128, 256, last=True)
-        add_up(5, 0, 128)
-        weigh(6, 0, 128)
-        add_up(6, 0, 128, last=True)
+        pick(1)
+        pick(3, 256, 512)
+        pick(3, 0, 256)
+        pick(0, 256, 512)
+        pick(0, 0, 256)
+        pick(2, 256, 512)
+        pick(2, 0, 256)
         pick(7, 0, 256)
+        fused(4)
+        add_up(4)
+        fused(5)
+        add_up(5)
+        weigh(1)
+        add_up(1)
+        weigh(3, 0, 256)
+        add_up(3, 0, 256)
+        weigh_pool(3, 256, 512)
+        add_up(3, 256, 512)
+        fused(6)
+        add_up(6)
+        weigh(0, 256, 512)
+        add_up(0, 256, 512)
+        weigh(2, 256, 512)
+        add_up(2, 256, 512, last=True)
+        weigh_pool(0, 0, 256)
+        add_up(0, 0, 256)
+        weigh(2, 0, 256)
+        add_up(2, 0, 256, last=True)
         turn_back(256, 512)
         turn_back(128, 256)
         turn_back(0, 128)
         fused(7, 256, 512)
+        weigh(7, 0, 256)
         finish(256, 512)
         store(256, 512)
-        weigh(7, 0, 256)
         finish(128, 256)
         store(128, 256)
         finish(0, 128)

@@ -6,8 +6,9 @@ from concourse.masks import make_identity
 K, T, D, V, M = 1024, 1024, 8, 512, 128
 P = 128
 PACK = 4
-K_PASS = P * PACK
-PASSES = K // K_PASS
+PASSES = K // (P * PACK)
+BLOCKS = V // P
+HALF = V // 2
 
 FLOPS = 2 * K * T * M + 2 * D * V * M
 
@@ -22,14 +23,15 @@ ADD = mybir.AluOpType.add
 IDENTITY = mybir.ActivationFunctionType.Identity
 COPY = mybir.ActivationFunctionType.Copy
 
-
-BANKS = ((0, 384), (384, 256), (640, 128), (768, 128), (896, 128))
-RANGES = ((0, 256), (256, 128), (384, 256), (640, 128), (768, 128), (896, 128))
-BLOCKS = V // P
-SPREAD = range(2, 14)
-ROW_STEP = 32 * V + P
-ENDS = ((256, 512), (128, 256), (0, 128))
+LATE_LOADS = ((0, 640), (640, 896), (896, T))
 UNITS = ((0, 0, 384), (0, 384, 256), (0, 640, 384), (1, 0, 384), (1, 384, 256), (1, 640, 256), (1, 896, 128))
+RANGES = {0: 256, 256: 128, 384: 256, 640: 128, 768: 128, 896: 128}
+BANKS = {0: 384, 384: 256, 640: 128, 768: 128, 896: 128}
+SPREAD = range(2, 14)
+SPREAD_BANKS = len(SPREAD) // BLOCKS
+ROW_STEP = 32 * V + P
+FIRST, LAST = 4, D - 1
+ENDS = (2, 3, 0, 1)
 
 
 def tile_picked_agg_lin_bias_sub_l_kernel(
@@ -45,261 +47,233 @@ def tile_picked_agg_lin_bias_sub_l_kernel(
         make_identity(nc, ident[:])
 
         x_rows = xT.rearrange("(c p j) t -> c p j t", c=PASSES, j=PACK)
-        w_rows = w.rearrange("(c p j) m -> p c j m", c=PASSES, j=PACK)
-        raws = []
+        raws = {}
 
-        def load_x(c, j0, j1, t0, t1):
-            raw = keep.tile([P, j1 - j0, t1 - t0], F32, name=f"raw{c}_{j0}_{t0}")
-            nc.sync.dma_start(out=raw[:], in_=x_rows[c][:, j0:j1, t0:t1])
-            raws.append((c, j0, j1, t0, t1, raw))
+        def load_x(c, t0, t1):
+            raws[c, t0, t1] = keep.tile([P, PACK, t1 - t0], F32, name=f"raw{c}_{t0}")
+            nc.sync.dma_start(out=raws[c, t0, t1][:], in_=x_rows[c][:, :, t0:t1])
 
-        w_raw = keep.tile([P, PASSES, PACK, M], F32, name="w_raw")
-        bias = keep.tile([P, 1], F32, name="bias")
+        load_x(0, 0, T)
 
-        def load_w():
-            nc.sync.dma_start(out=w_raw[:], in_=w_rows)
-
-        def load_bias():
-            nc.sync.dma_start(out=bias[:], in_=b)
-
-        load_x(0, 0, 4, 0, T)
         gate_rows = keep.tile([P, P], F32, name="gate_rows")
         nc.vector.memset(gate_rows[:], 0.0)
-        n_rows = len(SPREAD)
         flat = gate.rearrange("d p v -> (d p v)")[SPREAD[0] * ROW_STEP : (SPREAD[-1] + 1) * ROW_STEP]
-        nc.sync.dma_start(out=gate_rows[0:n_rows, :], in_=flat.rearrange("(i c) -> i c", c=ROW_STEP)[:, 0:P])
+        nc.sync.dma_start(out=gate_rows[0 : len(SPREAD), :], in_=flat.rearrange("(i c) -> i c", c=ROW_STEP)[:, 0:P])
         rows_turned = psum.tile([P, P], F32, name="rows_turned", tag="bank4")
         nc.tensor.transpose(rows_turned[:], gate_rows[:], ident[:])
-        gate_cols = keep.tile([P, n_rows], F32, name="gate_cols")
-        nc.scalar.copy(out=gate_cols[:], in_=rows_turned[:, 0:n_rows])
-        spread = [psum.tile([P, V], F32, name=f"spread{n}", tag=f"bank{5 + n}") for n in range(n_rows // BLOCKS)]
+        gate_cols = keep.tile([P, len(SPREAD)], F32, name="gate_cols")
+        nc.scalar.copy(out=gate_cols[:], in_=rows_turned[:, 0 : len(SPREAD)])
+        spread = [psum.tile([P, V], F32, name=f"spread{n}", tag=f"bank{len(BANKS) + n}") for n in range(SPREAD_BANKS)]
         for n, row in enumerate(SPREAD):
             d, i = divmod(row, BLOCKS)
-            col = gate_cols[:, n : n + 1]
-            nc.tensor.transpose(spread[d % 3][:, i * P : (i + 1) * P], col.to_broadcast([P, P]), ident[:])
+            column = gate_cols[:, n : n + 1].to_broadcast([P, P])
+            nc.tensor.transpose(spread[d % SPREAD_BANKS][:, i * P : (i + 1) * P], column, ident[:])
 
-        load_w()
-        load_x(1, 0, 4, 0, 640)
-        load_x(1, 0, 4, 640, 896)
-        load_x(1, 0, 4, 896, T)
-        load_bias()
-        offs = [keep.tile([P, V // 16], U16, name=f"off{d}") for d in range(D)]
-        gate_parts = []
+        w_raw = keep.tile([P, PASSES, PACK, M], F32, name="w_raw")
+        nc.sync.dma_start(out=w_raw[:], in_=w.rearrange("(c p j) m -> p c j m", c=PASSES, j=PACK))
+        for t0, t1 in LATE_LOADS:
+            load_x(1, t0, t1)
+        bias = keep.tile([P, 1], F32, name="bias")
+        nc.sync.dma_start(out=bias[:], in_=b)
+
+        offs, gates = {}, {}
 
         def load_list(d):
+            offs[d] = keep.tile([P, V // 16], U16, name=f"off{d}")
             nc.sync.dma_start(offs[d][:], lists[d])
 
-        def load_gate(d0, d1, lo=0, hi=V):
-            g = keep.tile([P, d1 - d0, hi - lo], F32, name=f"gate{d0}_{lo}")
-            nc.sync.dma_start(out=g[:], in_=gate[d0:d1, :, lo:hi].rearrange("d p v -> p d v"))
-            gate_parts.append((d0, d1, lo, hi, g))
+        def load_gate(d, lo=0, hi=V):
+            gates[d, lo] = keep.tile([P, hi - lo], F32, name=f"gate{d}_{lo}")
+            nc.sync.dma_start(out=gates[d, lo][:], in_=gate[d][:, lo:hi])
 
         def gate_of(d, lo, hi):
             if d * BLOCKS + lo // P in SPREAD:
-                return spread[d % 3][:, lo:hi]
-            d0, d1, v0, v1, g = [e for e in gate_parts if e[0] <= d < e[1] and e[2] <= lo < e[3]][0]
-            return g[:, d - d0, lo - v0 : hi - v0]
+                return spread[d % SPREAD_BANKS][:, lo:hi]
+            v0 = max(first for q, first in gates if q == d and first <= lo)
+            return gates[d, v0][:, lo - v0 : hi - v0]
 
-        load_list(4)
-        load_gate(4, 5)
-        load_list(5)
-        load_gate(5, 6)
+        for d in (4, 5):
+            load_list(d)
+            load_gate(d)
         load_list(1)
         load_list(3)
-        load_gate(3, 4, 256, 512)
+        load_gate(3, HALF, V)
         load_list(6)
-        load_gate(6, 7)
+        load_gate(6)
         load_list(0)
-        load_gate(0, 1, 0, 256)
+        load_gate(0, 0, HALF)
         load_list(2)
-        load_list(7)
-        load_gate(7, 8)
-
-        def interleave(copy, grouped, raw):
-            copy(
-                out=grouped.rearrange("p (g i) j -> p g j i", i=2),
-                in_=raw.rearrange("p j (g i) -> p g j i", i=2),
-            )
+        load_list(LAST)
+        load_gate(LAST, HALF, V)
+        load_gate(LAST, 0, HALF)
 
         y = keep.tile([P, T], F32, name="y")
-        w_grp = keep.tile([P, PASSES, M, PACK], BF16, name="w_grp", align_bytes=64)
+        w_woven = keep.tile([P, PASSES, M, PACK], BF16, name="w_woven", align_bytes=64)
         w_codes = keep.tile([P, PASSES * M], U32, name="w_codes", align_bytes=64)
         w_scales = keep.tile([P, PASSES * M], U8, name="w_scales", align_bytes=64)
-        grp, x_codes, x_scales = {}, {}, {}
+        woven, x_codes, x_scales = {}, {}, {}
         for c, t0, n in UNITS:
-            grp[c, t0] = keep.tile([P, n, PACK], BF16, name=f"grp{c}_{t0}", align_bytes=64)
+            woven[c, t0] = keep.tile([P, n, PACK], BF16, name=f"woven{c}_{t0}", align_bytes=64)
             x_codes[c, t0] = keep.tile([P, n], U32, name=f"x_codes{c}_{t0}", align_bytes=64)
             x_scales[c, t0] = keep.tile([P, n], U8, name=f"x_scales{c}_{t0}", align_bytes=64)
+        banks = {t0: psum.tile([P, n], F32, name=f"y{t0}", tag=f"bank{i}") for i, (t0, n) in enumerate(BANKS.items())}
 
         def part(tiles, c, lo, hi):
-            t0 = max(s for q, s, n in UNITS if q == c and s <= lo)
+            t0 = max(first for q, first, n in UNITS if q == c and first <= lo)
             return tiles[c, t0][:, lo - t0 : hi - t0]
 
-        banks = {}
-        for i, (t0, n) in enumerate(BANKS):
-            banks[t0] = psum.tile([P, n], F32, name=f"y{t0}", tag=f"bank{i}")
-
-        def quantize(c, t0, n):
-            nc.vector.quantize_mx(
-                out=part(x_codes, c, t0, t0 + n).bitcast(FP8X4),
-                scales=part(x_scales, c, t0, t0 + n),
-                in_=part(grp, c, t0, t0 + n).rearrange("p w j -> p (w j)"),
+        def weave(copy, c, lo, hi):
+            q, t0, t1 = [key for key in raws if key[0] == c and key[1] <= lo < key[2]][0]
+            copy(
+                out=part(woven, c, lo, hi).rearrange("p (g i) j -> p g j i", i=2),
+                in_=raws[q, t0, t1][:, :, lo - t0 : hi - t0].rearrange("p j (g i) -> p g j i", i=2),
             )
 
-        def quantize_w(c0, c1):
-            nc.vector.quantize_mx(
-                out=w_codes[:, c0 * M : c1 * M].bitcast(FP8X4),
-                scales=w_scales[:, c0 * M : c1 * M],
-                in_=w_grp[:, c0:c1].rearrange("p c m j -> p (c m j)"),
+        def weave_w(copy, c):
+            copy(
+                out=w_woven[:, c].rearrange("p (g i) j -> p g j i", i=2),
+                in_=w_raw[:, c].rearrange("p j (g i) -> p g j i", i=2),
             )
 
-        def multiply(c, r0):
-            hi = r0 + dict(RANGES)[r0]
-            t0, n = [e for e in BANKS if e[0] <= r0 < e[0] + e[1]][0]
+        def quantize(c, lo, hi):
+            nc.vector.quantize_mx(
+                out=part(x_codes, c, lo, hi).bitcast(FP8X4),
+                scales=part(x_scales, c, lo, hi),
+                in_=part(woven, c, lo, hi).rearrange("p n j -> p (n j)"),
+            )
+
+        def quantize_w(c):
+            nc.vector.quantize_mx(
+                out=w_codes[:, c * M : (c + 1) * M].bitcast(FP8X4),
+                scales=w_scales[:, c * M : (c + 1) * M],
+                in_=w_woven[:, c].rearrange("p m j -> p (m j)"),
+            )
+
+        def multiply(c, lo):
+            hi = lo + RANGES[lo]
+            t0 = max(first for first in BANKS if first <= lo)
             nc.tensor.matmul_mx(
-                out=banks[t0][:, r0 - t0 : hi - t0],
+                out=banks[t0][:, lo - t0 : hi - t0],
                 lhsT=w_codes[:, c * M : (c + 1) * M].bitcast(FP8X4),
                 lhsT_scale=w_scales[:, c * M : (c + 1) * M],
-                rhs=part(x_codes, c, r0, hi).bitcast(FP8X4),
-                rhs_scale=part(x_scales, c, r0, hi),
-                start=(c == 0 and r0 == t0),
-                stop=(c == PASSES - 1 and hi == t0 + n),
+                rhs=part(x_codes, c, lo, hi).bitcast(FP8X4),
+                rhs_scale=part(x_scales, c, lo, hi),
+                start=(c == 0 and lo == t0),
+                stop=(c == PASSES - 1 and hi == t0 + BANKS[t0]),
             )
 
-        def bring(t0):
-            n = dict(BANKS)[t0]
-            nc.scalar.activation(out=y[:, t0 : t0 + n], in_=banks[t0][:], func=IDENTITY, bias=bias[:])
+        def bring_scalar(t0):
+            nc.scalar.activation(out=y[:, t0 : t0 + BANKS[t0]], in_=banks[t0][:], func=IDENTITY, bias=bias[:])
 
-        def bring_vec(t0):
-            n = dict(BANKS)[t0]
-            nc.vector.tensor_scalar(out=y[:, t0 : t0 + n], in0=banks[t0][:], scalar1=bias[:], scalar2=None, op0=ADD)
-
-        def weave(copy, c, lo, hi, j=0):
-            c, j0, j1, t0, t1, raw = [r for r in raws if r[0] == c and r[1] == j and r[3] <= lo < r[4]][0]
-            interleave(copy, part(grp, c, lo, hi)[:, :, j0:j1], raw[:, :, lo - t0 : hi - t0])
-
-        def weave_w(copy, c0, c1):
-            copy(
-                out=w_grp[:, c0:c1].rearrange("p c (g i) j -> p c g j i", i=2),
-                in_=w_raw[:, c0:c1].rearrange("p c j (g i) -> p c g j i", i=2),
+        def bring_vector(t0):
+            nc.vector.tensor_scalar(
+                out=y[:, t0 : t0 + BANKS[t0]], in0=banks[t0][:], scalar1=bias[:], scalar2=None, op0=ADD
             )
 
         vec, sca = nc.vector.tensor_copy, nc.scalar.copy
-        weave(vec, 0, 0, 384)
+        weave(vec, 0, 0, 256)
+        weave(vec, 0, 256, 384)
         weave(sca, 0, 384, 640)
         weave(sca, 0, 640, 896)
         weave(vec, 0, 896, T)
-        quantize(0, 0, 256)
-        quantize(0, 256, 128)
-        weave_w(vec, 0, 1)
-        weave_w(sca, 1, 2)
-        quantize(0, 384, 256)
-        quantize_w(0, 1)
-        quantize(0, 896, 128)
-        quantize(0, 640, 256)
-        quantize_w(1, 2)
-        for r0, rn in RANGES:
-            multiply(0, r0)
+        for lo in (0, 128, 256):
+            quantize(0, lo, lo + P)
+        weave_w(vec, 0)
+        weave_w(sca, 1)
+        for lo in (384, 512):
+            quantize(0, lo, lo + P)
+        quantize_w(0)
+        for lo in (896, 640, 768):
+            quantize(0, lo, lo + P)
+        quantize_w(1)
+        for lo in RANGES:
+            multiply(0, lo)
+
         weave(vec, 1, 0, 256)
         weave(vec, 1, 384, 480)
         weave(sca, 1, 256, 384)
         weave(sca, 1, 480, 640)
         quantize(1, 0, 256)
-        quantize(1, 256, 128)
+        quantize(1, 256, 384)
         multiply(1, 0)
         multiply(1, 256)
-        quantize(1, 384, 256)
+        quantize(1, 384, 640)
         multiply(1, 384)
         weave(vec, 1, 640, 768)
         weave(sca, 1, 768, 896)
         weave(vec, 1, 896, T)
-        quantize(1, 640, 128)
-        multiply(1, 640)
-        quantize(1, 768, 128)
-        multiply(1, 768)
-        quantize(1, 896, 128)
-        multiply(1, 896)
-        bring(0)
-        bring(384)
-        bring_vec(640)
-        bring_vec(768)
-        bring(896)
+        for lo in (640, 768, 896):
+            quantize(1, lo, lo + P)
+            multiply(1, lo)
+        bring_scalar(0)
+        bring_scalar(384)
+        bring_vector(640)
+        bring_vector(768)
+        bring_scalar(896)
 
         prods = [keep.tile([P, V], F32, name=f"prod{d}") for d in range(D)]
-        picked = [keep.tile([P, V], F32, name=f"picked{d}") for d in range(D)]
-        accs = [psum.tile([P, P], F32, name=f"acc{i}", tag=f"bank{i}") for i in range(V // P)]
-        backs = {lo: psum.tile([P, hi - lo], F32, name=f"back{lo}", tag=f"bank{4 + h}") for h, (lo, hi) in enumerate(ENDS)}
+        picked = {d: keep.tile([P, V], F32, name=f"picked{d}") for d in (0, 1, 2, 3, LAST)}
+        sums = [psum.tile([P, P], F32, name=f"sum{i}", tag=f"bank{i}") for i in range(BLOCKS)]
+        backs = {i: psum.tile([P, P], F32, name=f"back{i}", tag=f"bank{BLOCKS + n}") for n, i in enumerate(ENDS)}
         turned = keep.tile([P, V], F32, name="turned")
         res = keep.tile([P, V], F32, name="res")
 
-        def fused(d, lo=0, hi=V):
-            nc.vector.tensor_tensor(
-                prods[d][:, lo:hi], y[:].indirect(offs[d][:, lo // 16 : hi // 16]), gate_of(d, lo, hi), MULT
-            )
+        def prod(d, lo, hi):
+            return (picked[3] if d == 0 and hi <= HALF else prods[d])[:, lo:hi]
+
+        def looked_up(d, lo, hi):
+            return y[:].indirect(offs[d][:, lo // 16 : hi // 16])
 
         def pick(d, lo=0, hi=V):
-            nc.scalar.activation(picked[d][:, lo:hi], y[:].indirect(offs[d][:, lo // 16 : hi // 16]), COPY)
+            nc.scalar.activation(picked[d][:, lo:hi], looked_up(d, lo, hi), COPY)
 
-        def weigh(d, lo=0, hi=V):
-            nc.vector.tensor_tensor(prods[d][:, lo:hi], picked[d][:, lo:hi], gate_of(d, lo, hi), MULT)
+        def fused(d, lo=0, hi=V):
+            nc.vector.tensor_tensor(prods[d][:, lo:hi], looked_up(d, lo, hi), gate_of(d, lo, hi), MULT)
 
-        def weigh_pool(d, lo, hi):
-            nc.gpsimd.tensor_tensor(prods[d][:, lo:hi], picked[d][:, lo:hi], gate_of(d, lo, hi), MULT)
+        def weigh(engine, d, lo=0, hi=V):
+            engine.tensor_tensor(prod(d, lo, hi), picked[d][:, lo:hi], gate_of(d, lo, hi), MULT)
 
         def add_up(d, lo=0, hi=V, last=False):
             for i in range(lo // P, hi // P):
-                nc.tensor.matmul(
-                    accs[i][:], prods[d][:, i * P : (i + 1) * P], ident[:], start=(d == 4), stop=last, is_transpose=True
-                )
-
-        def turn_back(lo, hi):
-            for v in range(lo, hi, P):
-                nc.scalar.copy(out=turned[:, v : v + P], in_=accs[v // P][:])
-            for v in range(lo, hi, P):
-                nc.tensor.transpose(backs[lo][:, v - lo : v - lo + P], turned[:, v : v + P], ident[:])
-
-        def finish(lo, hi):
-            nc.vector.tensor_tensor(res[:, lo:hi], prods[D - 1][:, lo:hi], backs[lo][:], ADD)
-
-        def store(lo, hi):
-            nc.sync.dma_start(out=out[:, lo:hi], in_=res[:, lo:hi])
+                block = prod(d, i * P, (i + 1) * P)
+                nc.tensor.matmul(sums[i][:], block, ident[:], start=(d == FIRST), stop=last, is_transpose=True)
 
         pick(1)
-        pick(3, 256, 512)
-        pick(3, 0, 256)
-        pick(0, 256, 512)
-        pick(0, 0, 256)
-        pick(2, 256, 512)
-        pick(2, 0, 256)
-        pick(7, 0, 256)
-        fused(4)
-        add_up(4)
-        fused(5)
-        add_up(5)
-        weigh(1)
+        for d in (3, 0, 2):
+            pick(d, HALF, V)
+            pick(d, 0, HALF)
+        pick(LAST, 0, HALF)
+
+        for d in (4, 5):
+            fused(d)
+            add_up(d)
+        weigh(nc.vector, 1)
         add_up(1)
-        weigh(3, 0, 256)
-        add_up(3, 0, 256)
-        weigh_pool(3, 256, 512)
-        add_up(3, 256, 512)
+        weigh(nc.vector, 3, 0, HALF)
+        add_up(3, 0, HALF)
+        weigh(nc.gpsimd, 3, HALF, V)
+        add_up(3, HALF, V)
+
         fused(6)
         add_up(6)
-        weigh(0, 256, 512)
-        add_up(0, 256, 512)
-        weigh(2, 256, 512)
-        add_up(2, 256, 512, last=True)
-        weigh_pool(0, 0, 256)
-        add_up(0, 0, 256)
-        weigh(2, 0, 256)
-        add_up(2, 0, 256, last=True)
-        turn_back(256, 512)
-        turn_back(128, 256)
-        turn_back(0, 128)
-        fused(7, 256, 512)
-        weigh(7, 0, 256)
-        finish(256, 512)
-        store(256, 512)
-        finish(128, 256)
-        store(128, 256)
-        finish(0, 128)
-        store(0, 128)
+        weigh(nc.vector, 0, HALF, V)
+        add_up(0, HALF, V)
+        weigh(nc.vector, 2, HALF, V)
+        add_up(2, HALF, V, last=True)
+        weigh(nc.gpsimd, 0, 0, HALF)
+        add_up(0, 0, HALF)
+        for lo in (0, P):
+            weigh(nc.vector, 2, lo, lo + P)
+            add_up(2, lo, lo + P, last=True)
+
+        for i in ENDS:
+            nc.scalar.copy(out=turned[:, i * P : (i + 1) * P], in_=sums[i][:])
+            nc.tensor.transpose(backs[i][:], turned[:, i * P : (i + 1) * P], ident[:])
+        fused(LAST, HALF, V)
+        weigh(nc.vector, LAST, 0, HALF)
+        for i in ENDS:
+            cols = slice(i * P, (i + 1) * P)
+            nc.vector.tensor_tensor(res[:, cols], prods[LAST][:, cols], backs[i][:], ADD)
+            if i % 2 == 1:
+                half = slice((i - 1) * P, (i + 1) * P)
+                nc.sync.dma_start(out=out[:, half], in_=res[:, half])

@@ -23,8 +23,8 @@ ADD = mybir.AluOpType.add
 IDENTITY = mybir.ActivationFunctionType.Identity
 COPY = mybir.ActivationFunctionType.Copy
 
-LATE_LOADS = ((0, 640), (640, 896), (896, T))
-UNITS = ((0, 0, 384), (0, 384, 256), (0, 640, 384), (1, 0, 384), (1, 384, 256), (1, 640, 256), (1, 896, 128))
+LATE_LOADS = ((0, 576), (576, 896), (896, T))
+UNITS = ((0, 0, 384), (0, 384, 256), (0, 640, 384), (1, 0, 384), (1, 384, 512), (1, 896, 128))
 RANGES = {0: 256, 256: 128, 384: 256, 640: 128, 768: 128, 896: 128}
 BANKS = {0: 384, 384: 256, 640: 128, 768: 128, 896: 128}
 SPREAD = range(2, 14)
@@ -50,7 +50,7 @@ def tile_picked_agg_lin_bias_sub_l_kernel(
         raws = {}
 
         def load_x(c, t0, t1):
-            raws[c, t0, t1] = keep.tile([P, PACK, t1 - t0], F32, name=f"raw{c}_{t0}")
+            raws[c, t0, t1] = keep.tile([P, PACK, t1 - t0], F32, name=f"raw{c}_{t0}", tag=f"raw{c}_{t0}")
             nc.sync.dma_start(out=raws[c, t0, t1][:], in_=x_rows[c][:, :, t0:t1])
 
         load_x(0, 0, T)
@@ -59,10 +59,12 @@ def tile_picked_agg_lin_bias_sub_l_kernel(
         nc.vector.memset(gate_rows[:], 0.0)
         flat = gate.rearrange("d p v -> (d p v)")[SPREAD[0] * ROW_STEP : (SPREAD[-1] + 1) * ROW_STEP]
         nc.sync.dma_start(out=gate_rows[0 : len(SPREAD), :], in_=flat.rearrange("(i c) -> i c", c=ROW_STEP)[:, 0:P])
+        nc.sync.dma_start(out=gate_rows[len(SPREAD) : len(SPREAD) + 1, :], in_=b.rearrange("m o -> o m"))
         rows_turned = psum.tile([P, P], F32, name="rows_turned", tag="bank4")
         nc.tensor.transpose(rows_turned[:], gate_rows[:], ident[:])
-        gate_cols = keep.tile([P, len(SPREAD)], F32, name="gate_cols")
-        nc.scalar.copy(out=gate_cols[:], in_=rows_turned[:, 0 : len(SPREAD)])
+        gate_cols = keep.tile([P, len(SPREAD) + 1], F32, name="gate_cols")
+        nc.scalar.copy(out=gate_cols[:], in_=rows_turned[:, 0 : len(SPREAD) + 1])
+        bias = gate_cols[:, len(SPREAD) : len(SPREAD) + 1]
         spread = [psum.tile([P, V], F32, name=f"spread{n}", tag=f"bank{len(BANKS) + n}") for n in range(SPREAD_BANKS)]
         for n, row in enumerate(SPREAD):
             d, i = divmod(row, BLOCKS)
@@ -73,8 +75,6 @@ def tile_picked_agg_lin_bias_sub_l_kernel(
         nc.sync.dma_start(out=w_raw[:], in_=w.rearrange("(c p j) m -> p c j m", c=PASSES, j=PACK))
         for t0, t1 in LATE_LOADS:
             load_x(1, t0, t1)
-        bias = keep.tile([P, 1], F32, name="bias")
-        nc.sync.dma_start(out=bias[:], in_=b)
 
         offs, gates = {}, {}
 
@@ -107,7 +107,6 @@ def tile_picked_agg_lin_bias_sub_l_kernel(
         load_gate(LAST, HALF, V)
         load_gate(LAST, 0, HALF)
 
-        y = keep.tile([P, T], F32, name="y")
         w_woven = keep.tile([P, PASSES, M, PACK], BF16, name="w_woven", align_bytes=64)
         w_codes = keep.tile([P, PASSES * M], U32, name="w_codes", align_bytes=64)
         w_scales = keep.tile([P, PASSES * M], U8, name="w_scales", align_bytes=64)
@@ -163,11 +162,11 @@ def tile_picked_agg_lin_bias_sub_l_kernel(
             )
 
         def bring_scalar(t0):
-            nc.scalar.activation(out=y[:, t0 : t0 + BANKS[t0]], in_=banks[t0][:], func=IDENTITY, bias=bias[:])
+            nc.scalar.activation(out=y[:, t0 : t0 + BANKS[t0]], in_=banks[t0][:], func=IDENTITY, bias=bias)
 
         def bring_vector(t0):
             nc.vector.tensor_scalar(
-                out=y[:, t0 : t0 + BANKS[t0]], in0=banks[t0][:], scalar1=bias[:], scalar2=None, op0=ADD
+                out=y[:, t0 : t0 + BANKS[t0]], in0=banks[t0][:], scalar1=bias, scalar2=None, op0=ADD
             )
 
         vec, sca = nc.vector.tensor_copy, nc.scalar.copy
@@ -180,8 +179,7 @@ def tile_picked_agg_lin_bias_sub_l_kernel(
             quantize(0, lo, lo + P)
         weave_w(vec, 0)
         weave_w(sca, 1)
-        for lo in (384, 512):
-            quantize(0, lo, lo + P)
+        quantize(0, 384, 640)
         quantize_w(0)
         for lo in (896, 640, 768):
             quantize(0, lo, lo + P)
@@ -190,21 +188,24 @@ def tile_picked_agg_lin_bias_sub_l_kernel(
             multiply(0, lo)
 
         weave(vec, 1, 0, 256)
-        weave(vec, 1, 384, 480)
+        weave(vec, 1, 384, 416)
         weave(sca, 1, 256, 384)
-        weave(sca, 1, 480, 640)
+        weave(sca, 1, 416, 576)
         quantize(1, 0, 256)
         quantize(1, 256, 384)
         multiply(1, 0)
         multiply(1, 256)
-        quantize(1, 384, 640)
+        quantize(1, 384, 512)
+        weave(vec, 1, 576, 704)
+        weave(sca, 1, 704, 896)
+        weave(vec, 1, 896, 960)
+        weave(sca, 1, 960, T)
+        quantize(1, 512, 640)
         multiply(1, 384)
-        weave(vec, 1, 640, 768)
-        weave(sca, 1, 768, 896)
-        weave(vec, 1, 896, T)
         for lo in (640, 768, 896):
             quantize(1, lo, lo + P)
             multiply(1, lo)
+        y = keep.tile([P, T], F32, name="y", tag="raw1_576")
         bring_scalar(0)
         bring_scalar(384)
         bring_vector(640)

@@ -92,10 +92,11 @@ def tile_picked_agg_lin_bias_sub_l_kernel(
             v0 = max(first for q, first in gates if q == d and first <= lo)
             return gates[d, v0][:, lo - v0 : hi - v0]
 
-        for d in (4, 5):
-            load_list(d)
-            load_gate(d)
+        load_list(4)
+        load_gate(4)
+        load_list(5)
         load_list(1)
+        load_gate(5)
         load_list(3)
         load_gate(3, HALF, V)
         load_list(6)

@@ -176,14 +176,14 @@ def tile_picked_agg_lin_bias_sub_l_kernel(
         weave(sca, 0, 384, 640)
         weave(sca, 0, 640, 896)
         weave(vec, 0, 896, T)
-        for lo in (0, 128, 256):
-            quantize(0, lo, lo + P)
+        quantize(0, 0, 256)
+        quantize(0, 256, 384)
         weave_w(vec, 0)
         weave_w(sca, 1)
         quantize(0, 384, 640)
         quantize_w(0)
-        for lo in (896, 640, 768):
-            quantize(0, lo, lo + P)
+        quantize(0, 896, T)
+        quantize(0, 640, 896)
         quantize_w(1)
         for lo in RANGES:
             multiply(0, lo)
@@ -221,7 +221,11 @@ def tile_picked_agg_lin_bias_sub_l_kernel(
         res = keep.tile([P, V], F32, name="res")
 
         def prod(d, lo, hi):
-            return (picked[3] if d == 0 and hi <= HALF else prods[d])[:, lo:hi]
+            if d == 3 and lo >= HALF:
+                return gate_of(5, lo, hi)
+            if d == 0 and hi <= HALF:
+                return gate_of(6, HALF + lo, HALF + hi)
+            return prods[d][:, lo:hi]
 
         def looked_up(d, lo, hi):
             return y[:].indirect(offs[d][:, lo // 16 : hi // 16])
@@ -240,15 +244,20 @@ def tile_picked_agg_lin_bias_sub_l_kernel(
                 block = prod(d, i * P, (i + 1) * P)
                 nc.tensor.matmul(sums[i][:], block, ident[:], start=(d == FIRST), stop=last, is_transpose=True)
 
+        def fused_in_halves(d):
+            for lo in (HALF, 0):
+                fused(d, lo, lo + HALF)
+                add_up(d, lo, lo + HALF)
+
         pick(1)
         for d in (3, 0, 2):
             pick(d, HALF, V)
             pick(d, 0, HALF)
         pick(LAST, 0, HALF)
 
-        for d in (4, 5):
-            fused(d)
-            add_up(d)
+        fused(4)
+        add_up(4)
+        fused_in_halves(5)
         weigh(nc.vector, 1)
         add_up(1)
         weigh(nc.vector, 3, 0, HALF)
@@ -256,8 +265,7 @@ def tile_picked_agg_lin_bias_sub_l_kernel(
         weigh(nc.gpsimd, 3, HALF, V)
         add_up(3, HALF, V)
 
-        fused(6)
-        add_up(6)
+        fused_in_halves(6)
         weigh(nc.vector, 0, HALF, V)
         add_up(0, HALF, V)
         weigh(nc.vector, 2, HALF, V)

@@ -23,10 +23,11 @@ ADD = mybir.AluOpType.add
 IDENTITY = mybir.ActivationFunctionType.Identity
 COPY = mybir.ActivationFunctionType.Copy
 
-LATE_LOADS = ((0, 576), (576, 896), (896, T))
-UNITS = ((0, 0, 384), (0, 384, 256), (0, 640, 384), (1, 0, 384), (1, 384, 512), (1, 896, 128))
-RANGES = {0: 256, 256: 128, 384: 256, 640: 128, 768: 128, 896: 128}
-BANKS = {0: 384, 384: 256, 640: 128, 768: 128, 896: 128}
+PAIR = 2
+LATE_LOADS = {0: 512, 512: 896, 896: T}
+UNITS = ((0, 0, 512), (0, 512, 512), (1, 0, 256), (1, 256, 256), (1, 512, 256), (1, 768, 128), (1, 896, 128))
+RANGES = {0: 256, 256: 256, 512: 128, 640: 128, 768: 128, 896: 128}
+BANKS = {0: 512, 512: 128, 640: 128, 768: 128, 896: 128}
 SPREAD = range(2, 14)
 SPREAD_BANKS = len(SPREAD) // BLOCKS
 ROW_STEP = 32 * V + P
@@ -47,13 +48,14 @@ def tile_picked_agg_lin_bias_sub_l_kernel(
         make_identity(nc, ident[:])
 
         x_rows = xT.rearrange("(c p j) t -> c p j t", c=PASSES, j=PACK)
-        raws = {}
+        whole = {}
 
-        def load_x(c, t0, t1):
-            raws[c, t0, t1] = keep.tile([P, PACK, t1 - t0], F32, name=f"raw{c}_{t0}", tag=f"raw{c}_{t0}")
-            nc.sync.dma_start(out=raws[c, t0, t1][:], in_=x_rows[c][:, :, t0:t1])
+        def load_rows(c, j, rows):
+            whole[c, j] = keep.tile([P, rows, T], F32, name=f"whole{c}_{j}")
+            nc.sync.dma_start(out=whole[c, j][:], in_=x_rows[c][:, j : j + rows, :])
 
-        load_x(0, 0, T)
+        load_rows(0, 0, PAIR)
+        load_rows(0, PAIR, PAIR)
 
         gate_rows = keep.tile([P, P], F32, name="gate_rows")
         nc.vector.memset(gate_rows[:], 0.0)
@@ -65,7 +67,7 @@ def tile_picked_agg_lin_bias_sub_l_kernel(
         gate_cols = keep.tile([P, len(SPREAD) + 1], F32, name="gate_cols")
         nc.scalar.copy(out=gate_cols[:], in_=rows_turned[:, 0 : len(SPREAD) + 1])
         bias = gate_cols[:, len(SPREAD) : len(SPREAD) + 1]
-        spread = [psum.tile([P, V], F32, name=f"spread{n}", tag=f"bank{len(BANKS) + n}") for n in range(SPREAD_BANKS)]
+        spread = [psum.tile([P, V], F32, name=f"spread{n}", tag=f"bank{5 + n}") for n in range(SPREAD_BANKS)]
         for n, row in enumerate(SPREAD):
             d, i = divmod(row, BLOCKS)
             column = gate_cols[:, n : n + 1].to_broadcast([P, P])
@@ -73,8 +75,11 @@ def tile_picked_agg_lin_bias_sub_l_kernel(
 
         w_raw = keep.tile([P, PASSES, PACK, M], F32, name="w_raw")
         nc.sync.dma_start(out=w_raw[:], in_=w.rearrange("(c p j) m -> p c j m", c=PASSES, j=PACK))
-        for t0, t1 in LATE_LOADS:
-            load_x(1, t0, t1)
+        load_rows(1, 0, 1)
+        late = {}
+        for t0, t1 in LATE_LOADS.items():
+            late[t0] = keep.tile([P, PACK - 1, t1 - t0], F32, name=f"late{t0}", tag=f"late{t0}")
+            nc.sync.dma_start(out=late[t0][:], in_=x_rows[1][:, 1:PACK, t0:t1])
 
         offs, gates = {}, {}
 
@@ -98,15 +103,17 @@ def tile_picked_agg_lin_bias_sub_l_kernel(
         load_list(1)
         load_gate(5)
         load_list(3)
-        load_gate(3, HALF, V)
+        both = keep.tile([P, 2, HALF], F32, name="gates03")
+        step = 3 * P * V + HALF
+        pair = gate.rearrange("d p v -> (d p v)")[0 : 2 * step].rearrange("(n s) -> n s", s=step)
+        nc.sync.dma_start(out=both[:], in_=pair[:, 0 : P * V].rearrange("n (p v) -> p n v", v=V)[:, :, 0:HALF])
+        gates[0, 0], gates[3, HALF] = both[:, 0], both[:, 1]
         load_list(6)
         load_gate(6)
         load_list(0)
-        load_gate(0, 0, HALF)
         load_list(2)
         load_list(LAST)
-        load_gate(LAST, HALF, V)
-        load_gate(LAST, 0, HALF)
+        load_gate(LAST)
 
         w_woven = keep.tile([P, PASSES, M, PACK], BF16, name="w_woven", align_bytes=64)
         w_codes = keep.tile([P, PASSES * M], U32, name="w_codes", align_bytes=64)
@@ -122,31 +129,24 @@ def tile_picked_agg_lin_bias_sub_l_kernel(
             t0 = max(first for q, first, n in UNITS if q == c and first <= lo)
             return tiles[c, t0][:, lo - t0 : hi - t0]
 
-        def weave(copy, c, lo, hi):
-            q, t0, t1 = [key for key in raws if key[0] == c and key[1] <= lo < key[2]][0]
-            copy(
-                out=part(woven, c, lo, hi).rearrange("p (g i) j -> p g j i", i=2),
-                in_=raws[q, t0, t1][:, :, lo - t0 : hi - t0].rearrange("p j (g i) -> p g j i", i=2),
-            )
+        def weave(copy, rows, places):
+            copy(out=places.rearrange("p (g i) j -> p g j i", i=2), in_=rows.rearrange("p j (g i) -> p g j i", i=2))
 
-        def weave_w(copy, c):
-            copy(
-                out=w_woven[:, c].rearrange("p (g i) j -> p g j i", i=2),
-                in_=w_raw[:, c].rearrange("p j (g i) -> p g j i", i=2),
-            )
+        def weave_pair(copy, j, lo, hi):
+            weave(copy, whole[0, j][:, :, lo:hi], part(woven, 0, lo, hi)[:, :, j : j + PAIR])
+
+        def weave_early(copy, lo, hi):
+            copy(out=part(woven, 1, lo, hi)[:, :, 0], in_=whole[1, 0][:, 0, lo:hi])
+
+        def weave_late(copy, lo, hi):
+            t0 = max(first for first in LATE_LOADS if first <= lo)
+            weave(copy, late[t0][:, :, lo - t0 : hi - t0], part(woven, 1, lo, hi)[:, :, 1:PACK])
 
         def quantize(c, lo, hi):
             nc.vector.quantize_mx(
                 out=part(x_codes, c, lo, hi).bitcast(FP8X4),
                 scales=part(x_scales, c, lo, hi),
                 in_=part(woven, c, lo, hi).rearrange("p n j -> p (n j)"),
-            )
-
-        def quantize_w(c):
-            nc.vector.quantize_mx(
-                out=w_codes[:, c * M : (c + 1) * M].bitcast(FP8X4),
-                scales=w_scales[:, c * M : (c + 1) * M],
-                in_=w_woven[:, c].rearrange("p m j -> p (m j)"),
             )
 
         def multiply(c, lo):
@@ -171,46 +171,46 @@ def tile_picked_agg_lin_bias_sub_l_kernel(
             )
 
         vec, sca = nc.vector.tensor_copy, nc.scalar.copy
-        weave(vec, 0, 0, 256)
-        weave(vec, 0, 256, 384)
-        weave(sca, 0, 384, 640)
-        weave(sca, 0, 640, 896)
-        weave(vec, 0, 896, T)
-        quantize(0, 0, 256)
-        quantize(0, 256, 384)
-        weave_w(vec, 0)
-        weave_w(sca, 1)
-        quantize(0, 384, 640)
-        quantize_w(0)
-        quantize(0, 896, T)
-        quantize(0, 640, 896)
-        quantize_w(1)
+        weave_pair(vec, 0, 0, 512)
+        weave_pair(sca, 0, 512, T)
+        for lo in (0, 256):
+            weave_pair(vec, PAIR, lo, lo + 256)
+            weave_pair(sca, PAIR, 512 + lo, 512 + lo + 256)
+        for lo in (0, 256, 512):
+            quantize(0, lo, lo + 256)
+        for c, copy in enumerate((vec, sca)):
+            weave(copy, w_raw[:, c], w_woven[:, c])
+        quantize(0, 768, T)
+        nc.vector.quantize_mx(
+            out=w_codes[:].bitcast(FP8X4), scales=w_scales[:], in_=w_woven[:].rearrange("p c m j -> p (c m j)")
+        )
         for lo in RANGES:
             multiply(0, lo)
 
-        weave(vec, 1, 0, 256)
-        weave(vec, 1, 384, 416)
-        weave(sca, 1, 256, 384)
-        weave(sca, 1, 416, 576)
-        quantize(1, 0, 256)
-        quantize(1, 256, 384)
-        multiply(1, 0)
-        multiply(1, 256)
-        quantize(1, 384, 512)
-        weave(vec, 1, 576, 704)
-        weave(sca, 1, 704, 896)
-        weave(vec, 1, 896, 960)
-        weave(sca, 1, 960, T)
-        quantize(1, 512, 640)
-        multiply(1, 384)
-        for lo in (640, 768, 896):
+        weave_early(vec, 0, 256)
+        weave_early(vec, 256, 320)
+        weave_early(sca, 320, 512)
+        weave_early(vec, 512, 768)
+        weave_early(sca, 768, 896)
+        weave_early(sca, 896, T)
+        weave_late(vec, 0, 256)
+        weave_late(vec, 256, 320)
+        weave_late(sca, 320, 512)
+        for lo in (0, 256):
+            quantize(1, lo, lo + 256)
+            multiply(1, lo)
+        weave_late(vec, 512, 640)
+        weave_late(vec, 640, 768)
+        weave_late(sca, 768, 896)
+        weave_late(sca, 896, T)
+        for lo in (512, 768, 640, 896):
             quantize(1, lo, lo + P)
             multiply(1, lo)
-        y = keep.tile([P, T], F32, name="y", tag="raw1_576")
+        y = keep.tile([P, T], F32, name="y", tag="late896")
         bring_scalar(0)
-        bring_scalar(384)
-        bring_vector(640)
+        bring_scalar(512)
         bring_vector(768)
+        bring_vector(640)
         bring_scalar(896)
 
         prods = [keep.tile([P, V], F32, name=f"prod{d}") for d in range(D)]
@@ -221,8 +221,6 @@ def tile_picked_agg_lin_bias_sub_l_kernel(
         res = keep.tile([P, V], F32, name="res")
 
         def prod(d, lo, hi):
-            if d == 3 and lo >= HALF:
-                return gate_of(5, lo, hi)
             if d == 0 and hi <= HALF:
                 return gate_of(6, HALF + lo, HALF + hi)
             return prods[d][:, lo:hi]
@@ -250,14 +248,17 @@ def tile_picked_agg_lin_bias_sub_l_kernel(
                 add_up(d, lo, lo + HALF)
 
         pick(1)
-        for d in (3, 0, 2):
-            pick(d, HALF, V)
-            pick(d, 0, HALF)
+        pick(3, HALF, V)
+        pick(3, 0, HALF)
+        pick(0)
+        pick(2, HALF, V)
+        pick(2, 0, HALF)
         pick(LAST, 0, HALF)
 
         fused(4)
         add_up(4)
-        fused_in_halves(5)
+        fused(5)
+        add_up(5)
         weigh(nc.vector, 1)
         add_up(1)
         weigh(nc.vector, 3, 0, HALF)

@@ -23,7 +23,6 @@ ADD = mybir.AluOpType.add
 IDENTITY = mybir.ActivationFunctionType.Identity
 COPY = mybir.ActivationFunctionType.Copy
 
-PAIR = 2
 LATE_LOADS = {0: 512, 512: 896, 896: T}
 UNITS = ((0, 0, 512), (0, 512, 512), (1, 0, 256), (1, 256, 256), (1, 512, 256), (1, 768, 128), (1, 896, 128))
 RANGES = {0: 256, 256: 256, 512: 128, 640: 128, 768: 128, 896: 128}
@@ -54,8 +53,7 @@ def tile_picked_agg_lin_bias_sub_l_kernel(
             whole[c, j] = keep.tile([P, rows, T], F32, name=f"whole{c}_{j}")
             nc.sync.dma_start(out=whole[c, j][:], in_=x_rows[c][:, j : j + rows, :])
 
-        load_rows(0, 0, PAIR)
-        load_rows(0, PAIR, PAIR)
+        load_rows(0, 0, PACK)
 
         gate_rows = keep.tile([P, P], F32, name="gate_rows")
         nc.vector.memset(gate_rows[:], 0.0)
@@ -113,7 +111,8 @@ def tile_picked_agg_lin_bias_sub_l_kernel(
         load_list(0)
         load_list(2)
         load_list(LAST)
-        load_gate(LAST)
+        load_gate(LAST, HALF, V)
+        load_gate(LAST, 0, HALF)
 
         w_woven = keep.tile([P, PASSES, M, PACK], BF16, name="w_woven", align_bytes=64)
         w_codes = keep.tile([P, PASSES * M], U32, name="w_codes", align_bytes=64)
@@ -132,8 +131,8 @@ def tile_picked_agg_lin_bias_sub_l_kernel(
         def weave(copy, rows, places):
             copy(out=places.rearrange("p (g i) j -> p g j i", i=2), in_=rows.rearrange("p j (g i) -> p g j i", i=2))
 
-        def weave_pair(copy, j, lo, hi):
-            weave(copy, whole[0, j][:, :, lo:hi], part(woven, 0, lo, hi)[:, :, j : j + PAIR])
+        def weave_first(copy, lo, hi):
+            weave(copy, whole[0, 0][:, :, lo:hi], part(woven, 0, lo, hi))
 
         def weave_early(copy, lo, hi):
             copy(out=part(woven, 1, lo, hi)[:, :, 0], in_=whole[1, 0][:, 0, lo:hi])
@@ -171,11 +170,9 @@ def tile_picked_agg_lin_bias_sub_l_kernel(
             )
 
         vec, sca = nc.vector.tensor_copy, nc.scalar.copy
-        weave_pair(vec, 0, 0, 512)
-        weave_pair(sca, 0, 512, T)
         for lo in (0, 256):
-            weave_pair(vec, PAIR, lo, lo + 256)
-            weave_pair(sca, PAIR, 512 + lo, 512 + lo + 256)
+            weave_first(vec, lo, lo + 256)
+            weave_first(sca, 512 + lo, 512 + lo + 256)
         for lo in (0, 256, 512):
             quantize(0, lo, lo + 256)
         for c, copy in enumerate((vec, sca)):

@@ -218,6 +218,8 @@ def tile_picked_agg_lin_bias_sub_l_kernel(
         res = keep.tile([P, V], F32, name="res")
 
         def prod(d, lo, hi):
+            if d == 3 and lo >= HALF:
+                return gate_of(5, lo, hi)
             if d == 0 and hi <= HALF:
                 return gate_of(6, HALF + lo, HALF + hi)
             return prods[d][:, lo:hi]
@@ -245,17 +247,14 @@ def tile_picked_agg_lin_bias_sub_l_kernel(
                 add_up(d, lo, lo + HALF)
 
         pick(1)
-        pick(3, HALF, V)
-        pick(3, 0, HALF)
-        pick(0)
-        pick(2, HALF, V)
-        pick(2, 0, HALF)
+        for d in (3, 0, 2):
+            pick(d, HALF, V)
+            pick(d, 0, HALF)
         pick(LAST, 0, HALF)
 
         fused(4)
         add_up(4)
-        fused(5)
-        add_up(5)
+        fused_in_halves(5)
         weigh(nc.vector, 1)
         add_up(1)
         weigh(nc.vector, 3, 0, HALF)

@@ -24,7 +24,7 @@ IDENTITY = mybir.ActivationFunctionType.Identity
 COPY = mybir.ActivationFunctionType.Copy
 
 LATE_LOADS = {0: 512, 512: 896, 896: T}
-UNITS = ((0, 0, 512), (0, 512, 512), (1, 0, 256), (1, 256, 256), (1, 512, 256), (1, 768, 128), (1, 896, 128))
+UNITS = ((0, 0, 512), (0, 512, 512), (1, 0, 512), (1, 512, 256), (1, 768, 128), (1, 896, 128))
 RANGES = {0: 256, 256: 256, 512: 128, 640: 128, 768: 128, 896: 128}
 BANKS = {0: 512, 512: 128, 640: 128, 768: 128, 896: 128}
 SPREAD = range(2, 14)
@@ -184,12 +184,12 @@ def tile_picked_agg_lin_bias_sub_l_kernel(
         for lo in RANGES:
             multiply(0, lo)
 
-        weave_early(vec, 0, 256)
-        weave_early(vec, 256, 320)
+        weave_early(vec, 0, 320)
         weave_early(sca, 320, 512)
         weave_early(vec, 512, 768)
         weave_early(sca, 768, 896)
-        weave_early(sca, 896, T)
+        weave_early(vec, 896, 960)
+        weave_early(sca, 960, T)
         weave_late(vec, 0, 256)
         weave_late(vec, 256, 320)
         weave_late(sca, 320, 512)
@@ -199,8 +199,11 @@ def tile_picked_agg_lin_bias_sub_l_kernel(
         weave_late(vec, 512, 640)
         weave_late(vec, 640, 768)
         weave_late(sca, 768, 896)
-        weave_late(sca, 896, T)
-        for lo in (512, 768, 640, 896):
+        quantize(1, 512, 640)
+        multiply(1, 512)
+        weave_late(vec, 896, 960)
+        weave_late(sca, 960, T)
+        for lo in (768, 640, 896):
             quantize(1, lo, lo + P)
             multiply(1, lo)
         y = keep.tile([P, T], F32, name="y", tag="late896")

@@ -24,7 +24,7 @@ IDENTITY = mybir.ActivationFunctionType.Identity
 COPY = mybir.ActivationFunctionType.Copy
 
 LATE_LOADS = {0: 512, 512: 896, 896: T}
-UNITS = ((0, 0, 512), (0, 512, 512), (1, 0, 512), (1, 512, 256), (1, 768, 128), (1, 896, 128))
+UNITS = ((0, 0, 512), (0, 512, 512), (1, 0, 512), (1, 512, 128), (1, 640, 384))
 RANGES = {0: 256, 256: 256, 512: 128, 640: 128, 768: 128, 896: 128}
 BANKS = {0: 512, 512: 128, 640: 128, 768: 128, 896: 128}
 SPREAD = range(2, 14)
@@ -186,9 +186,8 @@ def tile_picked_agg_lin_bias_sub_l_kernel(
 
         weave_early(vec, 0, 320)
         weave_early(sca, 320, 512)
-        weave_early(vec, 512, 768)
-        weave_early(sca, 768, 896)
-        weave_early(vec, 896, 960)
+        weave_early(vec, 640, 960)
+        weave_early(sca, 512, 640)
         weave_early(sca, 960, T)
         weave_late(vec, 0, 256)
         weave_late(vec, 256, 320)
@@ -196,21 +195,21 @@ def tile_picked_agg_lin_bias_sub_l_kernel(
         for lo in (0, 256):
             quantize(1, lo, lo + 256)
             multiply(1, lo)
-        weave_late(vec, 512, 640)
         weave_late(vec, 640, 768)
-        weave_late(sca, 768, 896)
-        quantize(1, 512, 640)
-        multiply(1, 512)
+        weave_late(vec, 768, 896)
+        weave_late(sca, 512, 640)
+        quantize(1, 640, 768)
+        multiply(1, 640)
         weave_late(vec, 896, 960)
         weave_late(sca, 960, T)
-        for lo in (768, 640, 896):
+        for lo in (512, 768, 896):
             quantize(1, lo, lo + P)
             multiply(1, lo)
         y = keep.tile([P, T], F32, name="y", tag="late896")
         bring_scalar(0)
-        bring_scalar(512)
+        bring_scalar(640)
+        bring_vector(512)
         bring_vector(768)
-        bring_vector(640)
         bring_scalar(896)
 
         prods = [keep.tile([P, V], F32, name=f"prod{d}") for d in range(D)]

from contextlib import ExitStack

import concourse.mybir as mybir
from concourse.masks import make_identity

K, T, D, V, M = 1024, 1024, 8, 512, 128
P = 128
PACK = 4
PASSES = K // (P * PACK)
BLOCKS = V // P
HALF = V // 2

FLOPS = 2 * K * T * M + 2 * D * V * M

F32 = mybir.dt.float32
BF16 = mybir.dt.bfloat16
U32 = mybir.dt.uint32
U16 = mybir.dt.uint16
U8 = mybir.dt.uint8
FP8X4 = mybir.dt.float8_e4m3fn_x4
MULT = mybir.AluOpType.mult
ADD = mybir.AluOpType.add
IDENTITY = mybir.ActivationFunctionType.Identity
COPY = mybir.ActivationFunctionType.Copy

LATE_LOADS = {0: 512, 512: 896, 896: T}
UNITS = ((0, 0, 512), (0, 512, 512), (1, 0, 512), (1, 512, 128), (1, 640, 384))
RANGES = {0: 256, 256: 256, 512: 128, 640: 128, 768: 128, 896: 128}
BANKS = {0: 512, 512: 128, 640: 128, 768: 128, 896: 128}
SPREAD = range(2, 14)
SPREAD_BANKS = len(SPREAD) // BLOCKS
ROW_STEP = 32 * V + P
FIRST, LAST = 4, D - 1
ENDS = (2, 3, 0, 1)


def tile_picked_agg_lin_bias_sub_l_kernel(
    tc, xT, w, b, gate, pos1, pos2, pos3, pos4, pos5, pos6, pos7, pos8, out
):
    nc = tc.nc
    lists = (pos1, pos2, pos3, pos4, pos5, pos6, pos7, pos8)
    with ExitStack() as ctx:
        keep = ctx.enter_context(tc.tile_pool(name="keep", bufs=1))
        psum = ctx.enter_context(tc.psum_pool(name="psum", bufs=1))

        ident = keep.tile([P, P], F32, name="ident")
        make_identity(nc, ident[:])

        x_rows = xT.rearrange("(c p j) t -> c p j t", c=PASSES, j=PACK)
        whole = {}

        def load_rows(c, j, rows):
            whole[c, j] = keep.tile([P, rows, T], F32, name=f"whole{c}_{j}")
            nc.sync.dma_start(out=whole[c, j][:], in_=x_rows[c][:, j : j + rows, :])

        load_rows(0, 0, PACK)

        gate_rows = keep.tile([P, P], F32, name="gate_rows")
        nc.vector.memset(gate_rows[:], 0.0)
        flat = gate.rearrange("d p v -> (d p v)")[SPREAD[0] * ROW_STEP : (SPREAD[-1] + 1) * ROW_STEP]
        nc.sync.dma_start(out=gate_rows[0 : len(SPREAD), :], in_=flat.rearrange("(i c) -> i c", c=ROW_STEP)[:, 0:P])
        nc.sync.dma_start(out=gate_rows[len(SPREAD) : len(SPREAD) + 1, :], in_=b.rearrange("m o -> o m"))
        rows_turned = psum.tile([P, P], F32, name="rows_turned", tag="bank4")
        nc.tensor.transpose(rows_turned[:], gate_rows[:], ident[:])
        gate_cols = keep.tile([P, len(SPREAD) + 1], F32, name="gate_cols")
        nc.scalar.copy(out=gate_cols[:], in_=rows_turned[:, 0 : len(SPREAD) + 1])
        bias = gate_cols[:, len(SPREAD) : len(SPREAD) + 1]
        spread = [psum.tile([P, V], F32, name=f"spread{n}", tag=f"bank{5 + n}") for n in range(SPREAD_BANKS)]
        for n, row in enumerate(SPREAD):
            d, i = divmod(row, BLOCKS)
            column = gate_cols[:, n : n + 1].to_broadcast([P, P])
            nc.tensor.transpose(spread[d % SPREAD_BANKS][:, i * P : (i + 1) * P], column, ident[:])

        w_raw = keep.tile([P, PASSES, PACK, M], F32, name="w_raw")
        nc.sync.dma_start(out=w_raw[:], in_=w.rearrange("(c p j) m -> p c j m", c=PASSES, j=PACK))
        load_rows(1, 0, 1)
        late = {}
        for t0, t1 in LATE_LOADS.items():
            late[t0] = keep.tile([P, PACK - 1, t1 - t0], F32, name=f"late{t0}", tag=f"late{t0}")
            nc.sync.dma_start(out=late[t0][:], in_=x_rows[1][:, 1:PACK, t0:t1])

        offs, gates = {}, {}

        def load_list(d):
            offs[d] = keep.tile([P, V // 16], U16, name=f"off{d}")
            nc.sync.dma_start(offs[d][:], lists[d])

        def load_gate(d, lo=0, hi=V):
            gates[d, lo] = keep.tile([P, hi - lo], F32, name=f"gate{d}_{lo}")
            nc.sync.dma_start(out=gates[d, lo][:], in_=gate[d][:, lo:hi])

        def gate_of(d, lo, hi):
            if d * BLOCKS + lo // P in SPREAD:
                return spread[d % SPREAD_BANKS][:, lo:hi]
            v0 = max(first for q, first in gates if q == d and first <= lo)
            return gates[d, v0][:, lo - v0 : hi - v0]

        load_list(4)
        load_gate(4)
        load_list(5)
        load_list(1)
        load_gate(5)
        load_list(3)
        both = keep.tile([P, 2, HALF], F32, name="gates03")
        step = 3 * P * V + HALF
        pair = gate.rearrange("d p v -> (d p v)")[0 : 2 * step].rearrange("(n s) -> n s", s=step)
        nc.sync.dma_start(out=both[:], in_=pair[:, 0 : P * V].rearrange("n (p v) -> p n v", v=V)[:, :, 0:HALF])
        gates[0, 0], gates[3, HALF] = both[:, 0], both[:, 1]
        load_list(6)
        load_gate(6)
        load_list(0)
        load_list(2)
        load_list(LAST)
        load_gate(LAST, HALF, V)
        load_gate(LAST, 0, HALF)

        w_woven = keep.tile([P, PASSES, M, PACK], BF16, name="w_woven", align_bytes=64)
        w_codes = keep.tile([P, PASSES * M], U32, name="w_codes", align_bytes=64)
        w_scales = keep.tile([P, PASSES * M], U8, name="w_scales", align_bytes=64)
        woven, x_codes, x_scales = {}, {}, {}
        for c, t0, n in UNITS:
            woven[c, t0] = keep.tile([P, n, PACK], BF16, name=f"woven{c}_{t0}", align_bytes=64)
            x_codes[c, t0] = keep.tile([P, n], U32, name=f"x_codes{c}_{t0}", align_bytes=64)
            x_scales[c, t0] = keep.tile([P, n], U8, name=f"x_scales{c}_{t0}", align_bytes=64)
        banks = {t0: psum.tile([P, n], F32, name=f"y{t0}", tag=f"bank{i}") for i, (t0, n) in enumerate(BANKS.items())}

        def part(tiles, c, lo, hi):
            t0 = max(first for q, first, n in UNITS if q == c and first <= lo)
            return tiles[c, t0][:, lo - t0 : hi - t0]

        def weave(copy, rows, places):
            copy(out=places.rearrange("p (g i) j -> p g j i", i=2), in_=rows.rearrange("p j (g i) -> p g j i", i=2))

        def weave_first(copy, lo, hi):
            weave(copy, whole[0, 0][:, :, lo:hi], part(woven, 0, lo, hi))

        def weave_early(copy, lo, hi):
            copy(out=part(woven, 1, lo, hi)[:, :, 0], in_=whole[1, 0][:, 0, lo:hi])

        def weave_late(copy, lo, hi):
            t0 = max(first for first in LATE_LOADS if first <= lo)
            weave(copy, late[t0][:, :, lo - t0 : hi - t0], part(woven, 1, lo, hi)[:, :, 1:PACK])

        def quantize(c, lo, hi):
            nc.vector.quantize_mx(
                out=part(x_codes, c, lo, hi).bitcast(FP8X4),
                scales=part(x_scales, c, lo, hi),
                in_=part(woven, c, lo, hi).rearrange("p n j -> p (n j)"),
            )

        def multiply(c, lo):
            hi = lo + RANGES[lo]
            t0 = max(first for first in BANKS if first <= lo)
            nc.tensor.matmul_mx(
                out=banks[t0][:, lo - t0 : hi - t0],
                lhsT=w_codes[:, c * M : (c + 1) * M].bitcast(FP8X4),
                lhsT_scale=w_scales[:, c * M : (c + 1) * M],
                rhs=part(x_codes, c, lo, hi).bitcast(FP8X4),
                rhs_scale=part(x_scales, c, lo, hi),
                start=(c == 0 and lo == t0),
                stop=(c == PASSES - 1 and hi == t0 + BANKS[t0]),
            )

        def bring_scalar(t0):
            nc.scalar.activation(out=y[:, t0 : t0 + BANKS[t0]], in_=banks[t0][:], func=IDENTITY, bias=bias)

        def bring_vector(t0):
            nc.vector.tensor_scalar(
                out=y[:, t0 : t0 + BANKS[t0]], in0=banks[t0][:], scalar1=bias, scalar2=None, op0=ADD
            )

        vec, sca = nc.vector.tensor_copy, nc.scalar.copy
        for lo in (0, 256):
            weave_first(vec, lo, lo + 256)
            weave_first(sca, 512 + lo, 512 + lo + 256)
        for lo in (0, 256, 512):
            quantize(0, lo, lo + 256)
        for c, copy in enumerate((vec, sca)):
            weave(copy, w_raw[:, c], w_woven[:, c])
        quantize(0, 768, T)
        nc.vector.quantize_mx(
            out=w_codes[:].bitcast(FP8X4), scales=w_scales[:], in_=w_woven[:].rearrange("p c m j -> p (c m j)")
        )
        for lo in RANGES:
            multiply(0, lo)

        weave_early(vec, 0, 320)
        weave_early(sca, 320, 512)
        weave_early(vec, 640, 960)
        weave_early(sca, 512, 640)
        weave_early(sca, 960, T)
        weave_late(vec, 0, 256)
        weave_late(vec, 256, 320)
        weave_late(sca, 320, 512)
        for lo in (0, 256):
            quantize(1, lo, lo + 256)
            multiply(1, lo)
        weave_late(vec, 640, 768)
        weave_late(vec, 768, 896)
        weave_late(sca, 512, 640)
        quantize(1, 640, 768)
        multiply(1, 640)
        weave_late(vec, 896, 960)
        weave_late(sca, 960, T)
        for lo in (512, 768, 896):
            quantize(1, lo, lo + P)
            multiply(1, lo)
        y = keep.tile([P, T], F32, name="y", tag="late896")
        bring_scalar(0)
        bring_scalar(640)
        bring_vector(512)
        bring_vector(768)
        bring_scalar(896)

        prods = [keep.tile([P, V], F32, name=f"prod{d}") for d in range(D)]
        picked = {d: keep.tile([P, V], F32, name=f"picked{d}") for d in (0, 1, 2, 3, LAST)}
        sums = [psum.tile([P, P], F32, name=f"sum{i}", tag=f"bank{i}") for i in range(BLOCKS)]
        backs = {i: psum.tile([P, P], F32, name=f"back{i}", tag=f"bank{BLOCKS + n}") for n, i in enumerate(ENDS)}
        turned = keep.tile([P, V], F32, name="turned")
        res = keep.tile([P, V], F32, name="res")

        def prod(d, lo, hi):
            if d == 3 and lo >= HALF:
                return gate_of(5, lo, hi)
            if d == 0 and hi <= HALF:
                return gate_of(6, HALF + lo, HALF + hi)
            return prods[d][:, lo:hi]

        def looked_up(d, lo, hi):
            return y[:].indirect(offs[d][:, lo // 16 : hi // 16])

        def pick(d, lo=0, hi=V):
            nc.scalar.activation(picked[d][:, lo:hi], looked_up(d, lo, hi), COPY)

        def fused(d, lo=0, hi=V):
            nc.vector.tensor_tensor(prods[d][:, lo:hi], looked_up(d, lo, hi), gate_of(d, lo, hi), MULT)

        def weigh(engine, d, lo=0, hi=V):
            engine.tensor_tensor(prod(d, lo, hi), picked[d][:, lo:hi], gate_of(d, lo, hi), MULT)

        def add_up(d, lo=0, hi=V, last=False):
            for i in range(lo // P, hi // P):
                block = prod(d, i * P, (i + 1) * P)
                nc.tensor.matmul(sums[i][:], block, ident[:], start=(d == FIRST), stop=last, is_transpose=True)

        def fused_in_halves(d):
            for lo in (HALF, 0):
                fused(d, lo, lo + HALF)
                add_up(d, lo, lo + HALF)

        pick(1)
        for d in (3, 0, 2):
            pick(d, HALF, V)
            pick(d, 0, HALF)
        pick(LAST, 0, HALF)

        fused(4)
        add_up(4)
        fused_in_halves(5)
        weigh(nc.vector, 1)
        add_up(1)
        weigh(nc.vector, 3, 0, HALF)
        add_up(3, 0, HALF)
        weigh(nc.gpsimd, 3, HALF, V)
        add_up(3, HALF, V)

        fused_in_halves(6)
        weigh(nc.vector, 0, HALF, V)
        add_up(0, HALF, V)
        weigh(nc.vector, 2, HALF, V)
        add_up(2, HALF, V, last=True)
        weigh(nc.gpsimd, 0, 0, HALF)
        add_up(0, 0, HALF)
        for lo in (0, P):
            weigh(nc.vector, 2, lo, lo + P)
            add_up(2, lo, lo + P, last=True)

        for i in ENDS:
            nc.scalar.copy(out=turned[:, i * P : (i + 1) * P], in_=sums[i][:])
            nc.tensor.transpose(backs[i][:], turned[:, i * P : (i + 1) * P], ident[:])
        fused(LAST, HALF, V)
        weigh(nc.vector, LAST, 0, HALF)
        for i in ENDS:
            cols = slice(i * P, (i + 1) * P)
            nc.vector.tensor_tensor(res[:, cols], prods[LAST][:, cols], backs[i][:], ADD)
            if i % 2 == 1:
                half = slice((i - 1) * P, (i + 1) * P)
                nc.sync.dma_start(out=out[:, half], in_=res[:, half])
